import numpy as np, ml_dtypes
CORES = [36,164,52,180,100,228,116,244]
N = 8
BF = ml_dtypes.bfloat16
A, W, HM, RO, MU = 1024, 2048, 2, 3, 4
n = A // 4
def view(j, c):
    return np.where(c < 0, W, (((c * (MU * j + 5)) >> 5) + 37 * j) & (W - 1))
def worth(tab, j, b):
    x = tab[:, view(j[None, :], b)]
    return np.add.reduce(np.maximum.accumulate(x[:, ::-1], axis=1)[:, ::-1], axis=0)
def pack(x, b, p):
    return {"sight": x.reshape(N, 128, W).astype(np.float32).astype(BF), "bun": np.ascontiguousarray(b.reshape(N, 128, A)).astype(np.int32), "pots": p.astype(np.int32)}
def looks(rng):
    return (rng.integers(0, 256, (N, 8, 16, W)) * rng.integers(1, 9, (N, 8, 1, W))) >> 3
def some(rng, goods, shares):
    return np.where(rng.random((N, 8, 16, A)) < rng.choice(np.array(shares), (N, 8, 1, A)), goods, -1)
def setup_inputs(rng):
    b = some(rng, rng.integers(0, 4096, (N, 8, 16, A)), [0.05, 0.2, 0.4, 0.7, 1.0])
    p = np.where(rng.random((N, 8, n)) < 0.85, rng.integers(0, 4096, (N, 8, n)), -1)
    return pack(looks(rng), b, p)
def setup_inputs_spread(rng):
    x = np.floor(np.exp2(8 * rng.random((N, 8, 1, W)) * rng.random((N, 8, 16, W)) ** 0.5)).astype(np.int64) - 1
    x = np.where(rng.random((N, 8, 16, W)) < 0.02, 255, np.clip(x, 0, 255))
    e = rng.choice(np.array([0.5, 1.0, 3.0, 6.0]), (N, 8, 1, A))
    b = some(rng, np.minimum((4096 * rng.random((N, 8, 16, A)) ** e).astype(np.int64), 4095), [0.05, 0.15, 0.5, 0.95])
    p = np.minimum((4096 * rng.random((N, 8, n)) ** rng.choice(np.array([0.3, 1.0, 4.0]), (N, 8, 1))).astype(np.int64), 4095)
    return pack(x, b, np.where(rng.random((N, 8, n)) < 0.9, p, -1))
def setup_inputs_ends(rng):
    see = view(np.arange(A), np.int64(4095))
    x = 255 * (rng.random((N, 8, 16, W)) < rng.choice(np.array([0.05, 0.3, 0.6, 0.95]), (N, 8, 1, W))).astype(np.int64)
    x[:, :, 0, see[0::4]] = 255
    far = np.array([0, A - 67, A - 66, A - 65, A - 4, A - 3, A - 2, A - 1]); x[..., see[far]] = 255
    b = some(rng, np.int64(4095), [0.0, 0.1, 0.5, 1.0])
    own = (rng.random((N, 8, 1, A)) < 0.33) & (np.arange(A) % 4 != 0)
    b = np.where(own, rng.integers(0, 4096, (N, 8, 16, A)), b)
    b[:, :, 3, 0::4] = 4095; b[..., 0] = 4095; b[..., A - 67:A - 64] = -1; b[..., A - 4] = -1
    end = np.where(rng.random((N, 8, 1, 3)) < 0.5, 4095, -1); end[N - 1, 7] = np.array([-1, 4095, -1]); end[0, 7] = np.array([-1, -1, 4095]); end[1, 7] = np.array([4095, -1, -1])
    b[..., A - 3:] = end
    p = np.where(rng.random((N, 8, n)) < 0.7, np.where(rng.random((N, 8, n)) < 0.6, 4095, -1), rng.integers(0, 4096, (N, 8, n)))
    p[..., 0] = 4095; p[..., n - 1] = 4095
    return pack(x, b, p)
def setup_inputs_corners(rng):
    x = looks(rng); b = rng.integers(0, 4096, (N, 8, 16, A)); p = rng.integers(0, 4096, (N, 8, n)); d = np.arange(16)[:, None]
    for r in range(N):
        mode = rng.permutation(8)
        for g in range(8):
            m = int(mode[g])
            if m == 0: b[r, g] = -1
            if m == 2: b[r, g, :15] = -1
            if m == 3: b[r, g, 1:] = -1
            if m == 4:
                c = int(b[r, g, 0, 0]); b[r, g] = np.where(rng.random((16, A)) < rng.random((1, A)), c, -1); p[r, g] = c
            if m == 5: b[r, g] = np.where(rng.random((1, A)) < 0.5, b[r, g], -1)
            if m == 6:
                k = rng.choice(np.array([0, 1, 15, 16]), (1, A)); low = rng.random((1, A)) < 0.5
                b[r, g] = np.where(np.where(low, d < k, d >= 16 - k), b[r, g], -1); p[r, g] = -1
            if m == 7: x[r, g] = 0
    return pack(x, b, p)
def calls(rng):
    return np.argsort(rng.random((N, 3, n)), axis=-1) + n * rng.integers(0, W // n, (N, 3, n))
def setup_inputs_ties(rng):
    base = rng.choice(np.array([0, 1, 127, 254]), (N, 8, 1, 1)); base[0, 0] = 0; base[0, 7] = 254; base[N - 1, 7] = 254
    x = base + (rng.random((N, 8, 16, W)) < 0.125)
    few = rng.integers(0, 4096, 32); few[0] = 0; few[1] = 4095
    b = some(rng, few[rng.integers(0, 32, (N, 8, 16, A))], [0.0, 0.1, 0.3, 0.6])
    p = np.where(rng.random((N, 8, n)) < 0.9, few[rng.integers(0, 32, (N, 8, n))], -1)
    full = rng.integers(0, 4096, (N, 16, A)); b3 = np.where(rng.random((N, 1, A)) < 0.5, full, -1)
    b3[:, :, 0::4] = full[:, :, 0::4]
    b3[:, 0:3, 0::4] = calls(rng)
    x[:, 3] = 100; b[:, 3] = b3
    for m in range(3):
        bm = rng.integers(0, 4096, (N, 16, A)); bm[:, 0:3, 0::4] = calls(rng); bm[:, :, m + 1::4] = -1
        x[:, 4 + m] = 100; b[:, 4 + m] = bm
    return pack(x, b, p)
def check_inputs(d):
    bad = []
    for k, lo, hi in (("sight", 0, 255), ("bun", -1, 4095), ("pots", -1, 4095)):
        v = np.asarray(d[k]).astype(np.float64)
        if not np.all((v >= lo) & (v <= hi) & (v == np.floor(v))): bad.append("range of " + k)
    return bad
def reference(sight, bun, pots):
    tab = np.zeros((N, 8, 16, W + 1), np.int32); tab[..., :W] = sight.astype(np.float32).reshape(N, 8, 16, W).astype(np.int32)
    bn = bun.astype(np.int64).reshape(N, 8, 16, A); p = pots.astype(np.int64); val = np.zeros((N, 8, A), np.int64)
    for r in range(N):
        for g in range(8): val[r, g] = worth(tab[r, g], np.arange(A), bn[r, g])[0]
    place = np.arange(16)[:, None]
    for t in range(RO):
        u = 4 * np.arange(n) + (t & 3); nbn = bn.copy(); nval = val.copy(); npots = np.zeros((N, 8, n), np.int64)
        for r in range(N):
            for g in range(8):
                old = bn[r, g][:, u]; s = old.copy(); s[15] = p[r, g]
                best = np.zeros(n, np.int64); who = np.full(n, -1); riv = []
                for m in range(3):
                    q = r if m < HM else (r + 1 + (t + m - HM) % (N - 1)) % N
                    j = 4 * ((old[m] + val[r, g, u] + 13 * t) & (n - 1)) + ((t + 1 + m) & 3)
                    first = np.zeros(n, bool); first[np.unique(j, return_index=True)[1]] = True
                    sv = worth(tab[q, g], j, s)
                    e = np.where(first, np.add.reduce((sv > val[q, g, j]).astype(np.int64), axis=0), 0)
                    who = np.where(e > best, m, who); best = np.maximum(best, e); riv.append((q, j, sv))
                new = s.copy()
                for m in range(3):
                    q, j, sv = riv[m]; c = np.flatnonzero(who == m); jc = j[c]
                    nbn[q, g][:, jc] = np.where(place >= best[c] - 1, s[:, c], -1); nval[q, g, jc] = sv[best[c] - 1, c]
                    new[:, c] = bn[q, g][:, jc]
                nbn[r, g][:, u] = new; nval[r, g, u] = worth(tab[r, g], u, new)[0]
                npots[(r + 1) % N, g] = np.where(best >= 2, s[np.maximum(best - 2, 0), np.arange(n)], old[15])
        bn, val, p = nbn, nval, npots
    return {"yb": bn.reshape(N, 128, A).astype(np.float32), "yv": val.astype(np.float32), "yp": p.astype(np.float32)}

@@ -1,0 +1,644 @@
+from concourse.mybir import AluOpType as O, ActivationFunctionType as F
+
+RO = 3
+f32, b16, i32, u16 = "float32", "bfloat16", "int32", "uint16"
+SCRATCH = {}
+
+
+def _b(name, cols, dtype, where="sbuf"):
+    SCRATCH[name] = (where, [128, cols], dtype)
+
+
+for _k in range(8):
+    _b("P%d" % _k, 512, f32, "psum")
+for _n, _c, _d in [
+    ("bunI", 1024, i32), ("potI", 256, i32), ("TB", 2064, b16), ("JC", 1024, f32), ("R01", 2048, b16),
+    ("ip", 128, i32), ("ic", 128, i32), ("id0", 128, i32), ("q1", 128, i32), ("q2", 128, i32), ("q3", 128, i32),
+    ("BM", 128, b16), ("BMq", 128, b16), ("BM8", 128, b16), ("DW", 128, b16), ("WX", 2048, b16), ("ONE", 256, b16),
+    ("cr", 512, b16), ("zr", 128, b16), ("r15", 128, b16), ("thb", 256, b16), ("THR", 256, f32),
+    ("SEL0", 128, f32), ("SEL1", 128, f32), ("SEL2", 128, f32), ("R15", 128, f32), ("NSH", 128, b16), ("BID", 128, b16),
+    ("k1", 128, b16), ("k2", 128, b16), ("rmask", 8, f32), ("wk", 16, i32), ("I1", 16, f32), ("I16", 16, f32), ("I8", 16, f32),
+    ("L0", 256, f32), ("V0L", 256, f32), ("BW", 12 * 256, f32), ("VW", 12 * 256, f32),
+    ("UB1", 512, f32), ("VB1", 512, f32), ("UB2", 256, f32), ("VB2", 256, f32),
+    ("P0in", 256, f32), ("Bz", 256, f32), ("DI", 256, i32), ("DIo", 256, i32), ("HB", 768, b16), ("Lf", 48, f32),
+    ("LV", 32, u16), ("p01", 32, f32), ("EB", 6528, b16), ("D8", 512, b16), ("D01", 512, b16),
+    ("VJ0", 256, f32), ("VJ1", 256, f32), ("VJ2", 256, f32), ("SMb", 8192, b16), ("SM2", 4096, b16), ("SMo", 4096, b16),
+    ("CM0", 512, b16), ("CM1", 256, b16), ("CMB", 256, b16), ("E02", 32, f32),
+    ("dec", 512, f32), ("IDX", 32, u16), ("Ys", 256, f32), ("SMg", 256, b16), ("VN", 256, f32), ("SMg2", 256, b16), ("VN2", 256, f32),
+    ("X2i", 32, u16), ("OFFO", 256, u16), ("OFFI", 1024, u16), ("OUT", 1024, f32), ("OUTV", 1024, f32), ("PO", 256, f32),
+]:
+    _b(_n, _c, _d)
+_b("GR", 4 * 4096, b16)
+for _k in range(4):
+    _b("h1_%d" % _k, 256, i32)
+for _k in range(3):
+    _b("h2_%d" % _k, 256, i32)
+for _k in range(2):
+    _b("OFF%d" % _k, 256, u16)
+for _k in range(RO):
+    _b("OS%d" % _k, 272, u16)
+    _b("OL%d" % _k, 272, u16)
+    _b("CS%d" % _k, 256, f32)
+    _b("KS%d" % _k, 256, b16)
+    _b("KL%d" % _k, 256, b16)
+    _b("XS%d" % _k, 288, f32)
+    _b("XL%d" % _k, 288, f32)
+    _b("PS%d" % _k, 256, f32)
+    _b("PL%d" % _k, 256, f32)
+SEMAPHORES = ["v", "s", "t", "gp", "ls"] + ["d%d" % k for k in range(10)] + ["%s%d" % (n, k) for n in ("ro", "rc", "rk", "rx", "rp") for k in range(RO)]
+CP = {"cy": 1.0e-3, "pe": 0.75e-3, "gat": 1.5, "sca": 3.5, "rem": 3.2, "lat": 0.15}
+BOOST = {'g0': 16.1, 'rk': 6.3, 'rp': 4.0, 'dd1': -2.3, 'ol0': 12.0, 'ol1': 19.3, 'io': 11.4, 'rx': 19.1, 'g2': 18.4, 'j11': 2.3, 'vj2': 13.6, 'rc': -7.1, 'cs': 7.4, 'ro': 6.3, 'dec0': 0.4, 'dd2': -1.0, 'const': -6.2, 'c0': 2.7, 'look0': 6.8, 'sc1': 9.8, 'j2': -1.1, 'dec1': -0.3, 'out': 1.6, 'init': 1.3, 'vj1': 4.3, 'look1': 0.6, 'own': 0.6, 'j10': 2.0, 'hc': -2.2}
+_order = {}
+
+
+def needs(ops):
+    n = len(ops)
+    dep = [set() for _ in range(n)]
+    hist = {}
+    for i, o in enumerate(ops):
+        if o["after"] is not None:
+            dep[i].add(o["after"])
+        for lst, w in ((o["ins"], False), (o["outs"], True)):
+            for x in lst:
+                nm, lo, hi = x[1], x[2], x[3]
+                if nm is None:
+                    continue
+                ps = SCRATCH[nm][0] == "psum" if nm in SCRATCH else False
+                for (l, h, w2, k) in hist.get(nm, ()):
+                    if k != i and ((w or w2) and l < hi and h > lo or ps and ops[k]["q"] != o["q"]):
+                        dep[i].add(k)
+        for lst, w in ((o["ins"], False), (o["outs"], True)):
+            for x in lst:
+                nm, lo, hi = x[1], x[2], x[3]
+                if nm is None:
+                    continue
+                if w:
+                    hist[nm] = [r for r in hist.get(nm, []) if not (r[0] >= lo and r[1] <= hi)]
+                hist.setdefault(nm, []).append((lo, hi, w, i))
+    return dep
+
+
+def arrange(ops, dep):
+    n = len(ops)
+    suc = [[] for _ in range(n)]
+    for i in range(n):
+        for k in dep[i]:
+            suc[k].append(i)
+    pr = [0.0] * n
+    for i in range(n - 1, -1, -1):
+        pr[i] = ops[i]["cost"] + ops[i]["lat"] + max([pr[k] for k in suc[i]] + [0.0]) + BOOST.get(ops[i]["tag"], 0.0)
+    left = [len(d) for d in dep]
+    rdy = [0.0] * n
+    free = {}
+    pool = {}
+    for i in range(n):
+        if not left[i]:
+            pool.setdefault(ops[i]["q"], []).append(i)
+    order = []
+    while len(order) < n:
+        best = None
+        for q, c in pool.items():
+            if not c:
+                continue
+            f = free.get(q, 0.0)
+            t = max(f, min(rdy[i] for i in c))
+            if best is None or t < best[0]:
+                k = max((i for i in c if rdy[i] <= t + 1e-9), key=lambda i: pr[i])
+                best = (t, q, k)
+        t, q, i = best
+        pool[q].remove(i)
+        order.append(i)
+        end = t + ops[i]["cost"]
+        free[q] = end if q != "R" else 0.0
+        for k in suc[i]:
+            rdy[k] = max(rdy[k], end + ops[i]["lat"])
+            left[k] -= 1
+            if not left[k]:
+                pool.setdefault(ops[k]["q"], []).append(k)
+    return order
+
+
+def rank_program(g, core, T, topo):
+    rank = T.rank_of(core)
+    if rank is None:
+        return
+    N = len(T.cores)
+    eng = {"V": g.vector, "S": g.scalar, "T": g.tensor, "Y": g.sync, "G": g}
+    own = {"V": "v", "S": "s", "T": "t", "G": "gp"}
+    cnt = {"v": 0, "s": 0, "t": 0, "gp": 0, "ls": 0}
+    know = {q: {} for q in eng}
+    recs = {}
+    nd = [0]
+    tag = [""]
+    ops = []
+    sent = {}
+
+    def A(n, lo=0, hi=None, st=1, ps=slice(None)):
+        if hi is None:
+            hi = T[n].shape[1]
+        return (T[n][ps, lo:hi:st], n, lo, hi)
+
+    def cols(x):
+        return x[0].shape[1]
+
+    def IND(w, o):
+        return (w[0].indirect(o[0]), [w, o])
+
+    def flat(lst):
+        out = []
+        for o in lst:
+            if isinstance(o[1], list):
+                out += o[1]
+            else:
+                out.append(o)
+        return out
+
+    def add(q, fns, outs, ins, cost, lat=None, after=None, kind="c"):
+        ops.append({"q": q, "fns": fns, "outs": flat(outs), "ins": flat(ins), "cost": cost, "lat": CP["lat"] if lat is None else lat,
+                    "after": after, "kind": kind, "tag": tag[0]})
+
+    def two(x):
+        return SCRATCH[x[1]][2] in (b16, u16)
+
+    def psum(x):
+        return SCRATCH[x[1]][0] == "psum"
+
+    def tt(o, a, b, op):
+        if isinstance(a[1], list):
+            c = 0.06 + 16 * cols(a[1][1]) * CP["gat"] * CP["cy"]
+        else:
+            c = max(64, cols(a) * (1 if psum(a) or psum(b) else 2)) * CP["cy"]
+        add("V", [lambda: g.vector.tensor_tensor(o[0], a[0], b[0], op)], [o], [a, b], c)
+
+    def ts(o, a, s1, op0, s2=None, op1=None):
+        x = [a] + [s for s in (s1,) if isinstance(s, tuple)]
+        v1 = s1[0] if isinstance(s1, tuple) else s1
+        c = max(64, cols(a) * (0.5 if two(o) and two(a) else 1)) * CP["cy"]
+        if op1 is None:
+            add("V", [lambda: g.vector.tensor_scalar(o[0], a[0], v1, None, op0)], [o], x, c)
+        else:
+            add("V", [lambda: g.vector.tensor_scalar(o[0], a[0], v1, s2, op0, op1)], [o], x, c)
+
+    def cp(o, a):
+        if isinstance(o[1], list):
+            c = 0.06 + 16 * cols(o[1][1]) * CP["sca"] * CP["cy"]
+        elif isinstance(a[1], list):
+            c = 0.06 + 16 * cols(a[1][1]) * CP["gat"] * CP["cy"]
+        else:
+            c = max(64, cols(a) * (0.5 if two(o) and two(a) else 1)) * CP["cy"]
+        add("V", [lambda: g.vector.tensor_copy(o[0], a[0])], [o], [a], c)
+
+    def fill(o, c):
+        add("V", [lambda: g.vector.memset(o[0], c)], [o], [], max(64, cols(o) * (0.5 if two(o) else 1)) * CP["cy"])
+
+    def act(o, a, scale=1.0):
+        c = 0.07 + 16 * cols(a[1][1]) * CP["gat"] * CP["cy"] if isinstance(a[1], list) else 0.1 + cols(a) * CP["cy"]
+        if isinstance(scale, tuple):
+            add("S", [lambda: g.scalar.activation(o[0], a[0], F.Copy, 0.0, scale[0])], [o], [a, scale], c)
+        else:
+            add("S", [lambda: g.scalar.activation(o[0], a[0], F.Copy)], [o], [a], c)
+
+    def mms(lst):
+        def one(x):
+            return lambda: g.tensor.matmul(x[0][0], x[1][0], x[2][0], x[3], x[4])
+        c = sum(max(64, cols(x[2])) * (1 if two(x[1]) else 4) for x in lst) * CP["pe"]
+        add("T", [one(x) for x in lst], [x[0] for x in lst], [y for x in lst for y in x[1:3]], c)
+
+    def mm(o, l, r, s, e):
+        mms([(o, l, r, s, e)])
+
+    def iota(o, pat, base, cm):
+        c = 0.15 + 2 * cols(o) * CP["cy"]
+        if SCRATCH[o[1]][2] != i32:
+            add("G", [lambda: g.iota(o[0], pat, base, cm, allow_small_or_imprecise_dtypes=True)], [o], [], c)
+        else:
+            add("G", [lambda: g.iota(o[0], pat, base, cm)], [o], [], c)
+
+    def dma(q, out, in_):
+        tag[0] = "io"
+        add(q, [lambda: eng[q].dma_start(out[0], in_[0])], [out] if out[1] else [], [in_] if in_[1] else [], 0.1, 3.0, None, "d")
+
+    def send(dst, out, in_, sem):
+        m = topo.mask(core, dst)
+        rid, pid = topo.addr(dst, core)
+        cnt["ls"] += len(topo.engines(core, dst))
+        sent[sem] = len(ops)
+        add("G", [lambda: g.remote_dma(out[0], in_[0], T.sem[sem], T.sem.ls, pid, rid, m)], [], [in_], 0.4, 0.0, None, "r")
+        ops[-1]["tag"] = sem[:2]
+
+    def recv(out, sem, src):
+        ne = len(topo.engines(src, core))
+        add("R", [(sem, ne)], [out], [], 0.0, CP["rem"], sent[sem], "v")
+
+    def wait_for(q, outs, ins):
+        need = []
+        for lst, w in ((ins, False), (outs, True)):
+            for o in lst:
+                n, lo, hi = o[1], o[2], o[3]
+                if n is None:
+                    continue
+                ps = SCRATCH[n][0] == "psum" if n in SCRATCH else False
+                for r in recs.get(n, ()):
+                    if r[3] == q:
+                        if q == "T" and ps:
+                            continue
+                        if (w or r[2]) and r[0] < hi and r[1] > lo:
+                            need.append(r)
+                    elif ps:
+                        need.append(r)
+                    elif r[0] < hi and r[1] > lo and (w or r[2]):
+                        need.append(r)
+        kn = know[q]
+        need = [r for r in need if kn.get(r[4], 0) < r[5]]
+        need.sort(key=lambda r: -sum(r[6].values()))
+        for r in need:
+            if kn.get(r[4], 0) < r[5]:
+                eng[q].wait_ge(T.sem[r[4]], r[5])
+                for s, v in r[6].items():
+                    if kn.get(s, 0) < v:
+                        kn[s] = v
+
+    def note(n, lo, hi, w, q, sem, val, clk):
+        if n is None:
+            return
+        if w:
+            recs[n] = [r for r in recs.get(n, []) if not (r[0] >= lo and r[1] <= hi)]
+        recs.setdefault(n, []).append((lo, hi, w, q, sem, val, clk))
+
+    def issue(o):
+        q = o["q"]
+        if o["kind"] == "v":
+            sem, ne = o["fns"][0]
+            cnt[sem] = ne
+            x = o["outs"][0]
+            note(x[1], x[2], x[3], True, "R", sem, ne, {sem: ne})
+            return
+        wait_for(q, o["outs"], o["ins"])
+        if o["kind"] == "r":
+            o["fns"][0]()
+            return
+        if o["kind"] == "d":
+            s, by = "d%d" % nd[0], "D"
+            nd[0] += 1
+            cnt[s] = 16
+            o["fns"][0]().then_inc(T.sem[s], 16)
+        else:
+            s, by = own[q], q
+            for f in o["fns"]:
+                cnt[s] += 1
+                f().then_inc(T.sem[s], 1)
+        clk = dict(know[q])
+        clk[s] = cnt[s]
+        for x in o["ins"]:
+            note(x[1], x[2], x[3], False, by, s, cnt[s], clk)
+        for x in o["outs"]:
+            note(x[1], x[2], x[3], True, by, s, cnt[s], clk)
+
+    def pull(off, lo, n, q="S", kind=0, at=None):
+        k = 4096 * kind + 16 * (lo if at is None else at)
+        o, w = A("GR", k, k + 16 * n), IND(A("TB"), A(off, lo, lo + n))
+        if q == "S":
+            act(o, w)
+        else:
+            cp(o, w)
+        return k
+
+    def scan(n, lo, k, m):
+        e = lo + 16 * m
+        o = (T[n][:, e - 1:(lo - 1 if lo else None):-1], n, lo, e)
+        d = (T.GR[:, k + 16 * m - 1:(k - 1 if k else None):-1], "GR", k, k + 16 * m)
+        z = (T.R01[:, 16 * m - 1::-1], "R01", 0, 16 * m)
+        add("V", [lambda: g.vector.tensor_tensor_scan(o[0], z[0], d[0], 0.0, O.mult, O.max)], [o], [z, d], 8 * m * CP["cy"])
+
+    dma("Y", A("bunI"), (T.bun[:], None, 0, 0))
+    dma("S", A("TB", 37, 2048), (T.sight[:, 0:2011], None, 0, 0))
+    dma("S", A("TB", 0, 37), (T.sight[:, 2011:2048], None, 0, 0))
+    fill(A("potI"), -1)
+    dma("Y", (T.potI[15::16, :], "potI", 0, 256), (T.pots[:], None, 0, 0))
+    iota(A("JC"), [[1, 4], [4, 256]], 1, 0)
+    iota(A("ip"), [[0, 128]], 0, 1)
+    iota(A("ic"), [[1, 128]], 0, 0)
+    iota(A("id0"), [[-1, 128]], 0, 1)
+    iota(A("wk"), [[16, 16]], 0, 0)
+    tag[0] = "const"
+    fill(A("TB", 2048, 2064), 0.0)
+    fill(A("R01"), 1.0)
+    fill(A("R01", 15, 2048, 16), 0.0)
+    fill(A("ONE"), 1.0)
+    fill(A("WX"), 0.0)
+    for y in range(16):
+        fill(A("thb", y, 256, 16), 2.0 ** -y)
+    for s in range(4):
+        fill(A("cr", 128 * s, 128 * s + 128), float(s + 1))
+    fill(A("zr"), 0.0)
+    fill(A("r15"), 0.0)
+    fill(A("r15", 15, 128, 16), 1.0)
+    ts(A("q1"), A("ip"), 4, O.arith_shift_right)
+    ts(A("q2"), A("ic"), 4, O.arith_shift_right)
+    tt(A("BM"), A("q1"), A("q2"), O.is_equal)
+    ts(A("q3"), A("ip"), 15, O.bitwise_and)
+    for gg in range(8):
+        ts(A("WX", 16 * gg, 16 * gg + 15 * 129 + 1, 129), A("ONE", 0, 16), A("BM", 16 * gg, 16 * gg + 1), O.mult)
+
+    def W(y):
+        return A("WX", 128 * y, 128 * y + 128)
+
+    ts(A("BMq"), A("BM"), 0.25, O.mult)
+    ts(A("BM8"), A("BM"), 8.0, O.mult)
+    for m in range(3):
+        ts(A("k1"), A("q3"), m, O.is_equal)
+        tt(A("SEL%d" % m), A("k1"), A("BM"), O.mult)
+    ts(A("rmask", 0, 1), A("q3", 0, 1), 15, O.not_equal)
+    cp(A("R15"), W(15))
+    ts(A("k1"), A("id0"), 1, O.is_equal)
+    tt(A("k1"), A("k1"), A("BM"), O.mult)
+    ts(A("NSH"), A("k1"), -1.0, O.mult)
+    ts(A("k2"), A("id0"), 2, O.is_equal)
+    tt(A("k2"), A("k2"), A("BM"), O.mult)
+    tt(A("k1"), A("k1"), A("k2"), O.subtract)
+    ts(A("k2"), A("q3"), 1, O.is_equal)
+    tt(A("k2"), A("k2"), W(15), O.mult)
+    tt(A("BID"), A("k1"), A("k2"), O.subtract)
+    tt(A("I1"), A("q3", 0, 16), A("wk"), O.add)
+    ts(A("I16"), A("I1"), 16.0, O.mult)
+    for h in range(2):
+        cp(A("I8", 8 * h, 8 * h + 8), A("I16", 0, 8))
+    ts(A("THR"), A("thb"), 2.0, O.mult)
+    mm(A("P4", 0, 128), A("thb", 0, 128, 1, slice(0, 1)), A("ONE", 0, 128, 1, slice(0, 1)), True, True)
+    tt(A("DW"), A("P4", 0, 128), A("BM"), O.mult)
+    ONE1 = A("ONE", 0, 256, 1, slice(0, 1))
+    ONEh = A("ONE", 0, 128, 1, slice(0, 1))
+    iota(A("BW", 1536, 1792), [[0, 256]], 0, 0)
+    iota(A("BW", 2304, 2560), [[0, 256]], 0, 0)
+
+    def goods(o, src, pt):
+        ts(pt, src, 0, O.is_ge, 296.0, O.mult)
+        tt(o, pt, src, O.add)
+
+    def look(o, D, c, J, k):
+        h1 = A("h1_%d" % k, 0, cols(c))
+        tt(h1, c, J, O.mult)
+        tt(h1, h1, D, O.add)
+        ts(h1, h1, 3, O.arith_shift_right, 2047 | (1 << 20), O.bitwise_and)
+        ts(o, h1, 2048, O.min)
+
+    def quarter(o, c):
+        ts(o, c, 0.25, O.mult, -74.375, O.add)
+
+    def worth(off, lo, dst, at, n, q="S"):
+        tag[0] = "own"
+        k = pull(off, lo, n, q, 3, at)
+        scan("SMo", 16 * at, k, n)
+        mm(A("P7", at, at + n), A("BM"), A("SMo", 16 * at, 16 * at + 16 * n, 16), True, True)
+        act(dst, A("P7", at, at + n))
+
+    BWc = {1: ("BW", 512), 2: ("BW", 768), 3: ("BW", 1792), 0: ("L0", 0)}
+    VWc = {1: ("VW", 512), 2: ("VW", 768), 3: ("VW", 1792), 0: ("V0L", 0)}
+
+    def sub(x, lo, hi):
+        return A(x[0], x[1] + lo, x[1] + hi)
+    act(A("P5"), A("JC", 0, 512))
+    act(A("P6"), A("JC", 512, 1024))
+    tag[0] = "init"
+    for s in range(4):
+        goods(sub(BWc[s], 0, 256), A("bunI", s, 1024, 4), A("P%d" % s, 0, 256))
+        quarter(A("DIo"), sub(BWc[s], 0, 256))
+        look(A("OFFI", 256 * s, 256 * s + 256), A("DIo"), sub(BWc[s], 0, 256), A("P%d" % (5 + s // 2), 256 * (s % 2), 256 * (s % 2) + 256), s)
+    goods(A("P0in"), A("potI"), A("P4", 0, 256))
+
+    def first_worth(s):
+        for h in range(2):
+            worth("OFFI", 256 * s + 128 * h, sub(VWc[s], 128 * h, 128 * h + 128), 128 * h, 128)
+    first_worth(0)
+    first_worth(1)
+
+    wins = [(0, 1024, 0, 512, 768), (768, 2048, 256, 0, 1024), (1792, 3072, 768, 0, 256)]
+    Sblk = [0, 1024, 2560]
+    hostw = [("BW", "VW", 1536, 2048, 256, 0), ("BW", "VW", 2048, 2560, 0, 256), ("UB1", "VB1", 0, 512, 0, 256)]
+    lead = [(("L0", 0), ("V0L", 0)), (("BW", 512), ("VW", 512)), (("BW", 768), ("VW", 768))]
+    newl = [(("BW", 2048), ("VW", 2048)), (("UB1", 0), ("VB1", 0)), (("UB2", 0), ("VB2", 0))]
+    nxt, prv = T.cores[(rank + 1) % N], T.cores[(rank - 1) % N]
+
+    def DC(k, w=16):
+        return A("dec", 16 * k, 16 * k + w)
+
+    def wrap(at, src, lo, k0=0, k1=16):
+        mms([(A("P6", at + k0, at + k1), W(y), A(src, lo + 16 * k0 + y, lo + 16 * k1, 16), y == 0, y == 15) for y in range(16)])
+
+    def judge(bank, at, smn, lo, n, k):
+        scan(smn, lo, k, n)
+        mms([(A(bank, at, at + n), W(d), A(smn, lo + d, lo + 16 * n, 16), d == 0, d == 15) for d in range(16)])
+
+    def dedup(m):
+        base = 2176 * m
+        o = [base + sum(256 - 16 * j for j in range(k)) for k in range(17)]
+        for k in range(16):
+            ts(A("EB", o[k], o[k + 1]), A("HB", 256 * m + 16 * k, 256 * m + 256), A("Lf", 16 * m + k, 16 * m + k + 1), O.is_equal)
+        P = "P%d" % m
+        l = [(A(P, 0, 256), A("zr", 0, 128, 1, slice(0, 1)), ONE1, True, False)]
+        for k in range(16):
+            if k < 15:
+                l.append((A(P, 16 * k + 16, 256), A("BM8"), A("EB", o[k] + 16, o[k + 1]), False, False))
+            l.append((A(P, 16 * k, 16 * k + 16), A("DW"), A("EB", o[k], o[k] + 16), False, k == 15))
+        for a in range(0, len(l), 4):
+            mms(l[a:a + 4])
+
+    def host_change(t):
+        bw, vw, a, e, cb, db = hostw[t]
+        recv(A("XL%d" % t), "rx%d" % t, T.cores[(rank - 1 - t) % N])
+        tag[0] = "hc"
+        cp(A("X2i"), A("XL%d" % t, 256, 288))
+        act(A("SMg2"), IND(A("SM2"), A("X2i", 16, 32)))
+        mm(A("P7", 256, 512), A("BM"), A("SMg2"), True, True)
+        act(A("VN2"), A("P7", 256, 512))
+        cp(IND(A(bw, a, e), A("X2i", 0, 16)), A("XL%d" % t, 0, 256))
+        cp(IND(A(vw, a, e), A("X2i", 0, 16)), A("VN2"))
+
+    for t in range(RO):
+        q, p = T.cores[(rank + 1 + t) % N], T.cores[(rank - 1 - t) % N]
+        LB, LVv = sub(lead[t][0], 0, 256), sub(lead[t][1], 0, 256)
+        wa, we, so, c0, c1 = wins[t]
+        S = A("BW", Sblk[t], Sblk[t] + 256)
+        if t == 0:
+            pool = A("P0in")
+        else:
+            pool = A("PL%d" % (t - 1))
+            recv(pool, "rp%d" % (t - 1), prv)
+        tag[0] = "hash"
+        ts(A("Bz"), LB, 39.0, O.max, 13.0 * t + 216.0, O.add)
+        act(A("P5", 0, 256), LB, A("rmask", 0, 1))
+        for m in (0, 2, 1):
+            h1, h2, HBm = A("h1_%d" % m), A("h2_%d" % m), A("HB", 256 * m, 256 * m + 256)
+            P = "P%d" % m
+            mm(A(P, 0, 256), A("SEL%d" % m), A("Bz"), True, True)
+            tt(h1, A(P, 0, 256), LVv, O.add)
+            ts(h2, h1, 255, O.bitwise_and)
+            cp(HBm, h2)
+            s = (t + 1 + m) & 3
+            mms([(A(P, 256, 512), A("cr", 128 * s, 128 * s + 128, 1, slice(0, 1)), ONE1, True, False),
+                 (A(P, 256, 512), A("BMq"), HBm, False, True)])
+        tt(S, A("P5", 0, 256), pool, O.max)
+        quarter(A("DI"), S)
+        PD = A("P5", 256, 512)
+        mms([(A("P6", 0, 48), W(y), A("HB", y, 768, 16), y == 0, y == 15) for y in range(16)])
+        ts(A("Lf"), A("P6", 0, 48), 0.0625, O.mult)
+        cp(PD, A("DI"))
+        OS, OL = "OS%d" % t, "OL%d" % t
+        for m in (0, 2, 1):
+            J = A("P%d" % m, 256, 512)
+            tag[0] = "look%d" % m
+            look(A(OS, 0, 256) if m == 2 else A("OFF%d" % m), PD, S, J, m)
+            if m == 2:
+                cp(A(OS, 256, 272), A("Lf", 32, 48))
+                send(q, A(OL), A(OS), "ro%d" % t)
+        tag[0] = "g0"
+        k0 = [pull("OFF0", 128 * h, 128) for h in range(2)]
+        ts(A("p01", 0, 16), A("Lf", 0, 16), float(c0), O.add)
+        ts(A("p01", 16, 32), A("Lf", 16, 32), float(c1), O.add)
+        cp(A("LV"), A("Lf", 0, 32))
+        tag[0] = "dd0"
+        dedup(0)
+        tag[0] = "j0"
+        for h in range(2):
+            judge("P3", 128 * h, "SMb", 4096 * h, 128, k0[h])
+        if t == 0:
+            first_worth(3)
+        bw, vw, ha, he, hcb, hdb = hostw[t]
+        recv(A(OL), "ro%d" % t, p)
+        tag[0] = "cs"
+        clsB, clsV = A(bw, ha + hcb, ha + hcb + 256), A(vw, ha + hcb, ha + hcb + 256)
+        act(A("CS%d" % t), IND(clsB, A(OL, 256, 272)))
+        send(p, A("BW", Sblk[t] + 256, Sblk[t] + 512), A("CS%d" % t), "rc%d" % t)
+        tag[0] = "g2"
+        k2 = [pull(OL, 128 * h, 128, "S", 2) for h in range(2)]
+        tag[0] = "vj2"
+        act(A("VJ2"), IND(clsV, A(OL, 256, 272)))
+        tag[0] = "c0"
+        tt(A("D01", 0, 256), A("P0", 0, 256), A("THR"), O.is_ge)
+        ts(A("D8", 0, 256), A("D01", 0, 256), 8192.0, O.mult)
+        tt(A("VJ0"), IND(A("VW", wa + c0, wa + c0 + 256), A("LV", 0, 16)), A("D8", 0, 256), O.add)
+        tt(A("CM0", 0, 256), A("P3", 0, 256), A("VJ0"), O.is_gt)
+        act(A("P0", 0, 256), A("CM0", 0, 256))
+        if t > 0:
+            host_change(t - 1)
+        tag[0] = "j2"
+        for h in range(2):
+            judge("P5", 128 * h, "SM2", 2048 * h, 128, k2[h])
+        tt(A("KS%d" % t), A("P5", 0, 256), A("VJ2"), O.is_gt)
+        send(p, A("KL%d" % t), A("KS%d" % t), "rk%d" % t)
+        tag[0] = "dd1"
+        dedup(1)
+        tag[0] = "dd2"
+        dedup(2)
+        tt(A("D01", 256, 512), A("P1", 0, 256), A("THR"), O.is_ge)
+        ts(A("D8", 256, 512), A("D01", 256, 512), 8192.0, O.mult)
+        if t == 0:
+            first_worth(2)
+        tag[0] = "vj1"
+        tt(A("VJ1"), IND(A("VW", wa + c1, wa + c1 + 256), A("LV", 16, 32)), A("D8", 256, 512), O.add)
+        tt(A("P2", 256, 512), A("P2", 0, 256), A("THR"), O.is_lt)
+        recv(A("KL%d" % t), "rk%d" % t, q)
+        tag[0] = "pre"
+        tt(A("CM0", 256, 512), A("KL%d" % t), A("P2", 256, 512), O.mult)
+        mms([(A("P6", 64, 96), W(y), A("CM0", y, 512, 16), y == 0, y == 15) for y in range(16)])
+        tt(A("P0", 0, 256), A("P0", 0, 256), A("CM0", 256, 512), O.max)
+        act(A("E02"), A("P6", 64, 96))
+        e0, e2 = A("E02", 0, 16), A("E02", 16, 32)
+        ts(DC(0), e0, 1.0, O.add)
+        tt(DC(0), DC(0), e2, O.max)
+        ts(DC(2), e0, 0.0, O.is_gt)
+        ts(DC(1), A("I1"), float(so), O.add)
+        tt(DC(3), A("p01", 0, 16), DC(1), O.subtract)
+        tt(DC(3), DC(3), DC(2), O.mult)
+        tt(DC(3), DC(3), DC(1), O.add)
+        tt(DC(4), e2, e0, O.is_gt)
+        ts(DC(1), DC(1), 256.0, O.add)
+        tt(DC(5), DC(1), DC(3), O.subtract)
+        tt(DC(5), DC(5), DC(4), O.mult)
+        tt(DC(5), DC(5), DC(3), O.add)
+        tt(DC(6), A("p01", 16, 32), DC(5), O.subtract)
+        ts(DC(7), e0, -1.0, O.add, 0.0, O.max)
+        tt(DC(7), DC(7), A("I8"), O.add)
+        tt(DC(8), A("I8"), DC(7), O.subtract)
+        ts(DC(8), DC(8), 2047.0, O.add)
+        ts(DC(9), A("I1"), float(hdb), O.add)
+        tt(DC(10), A("Lf", 32, 48), DC(9), O.subtract)
+        ts(DC(10), DC(10), float(hcb), O.add)
+        tt(DC(10), DC(10), DC(4), O.mult)
+        tt(DC(9), DC(9), DC(10), O.add)
+        ts(DC(11), e2, -1.0, O.add, 0.0, O.max)
+        XS = "XS%d" % t
+        tt(A(XS, 272, 288), DC(11), A("I16"), O.add)
+        win = A("BW", wa, we)
+        recv(A("BW", Sblk[t] + 256, Sblk[t] + 512), "rc%d" % t, q)
+        for h in range(2):
+            lo, hi, bank, fb = 128 * h, 128 * h + 128, ("P4", "P5")[h], ("P3", "P4")[h]
+            at = lo
+            tag[0] = "j1%d" % h
+            for n in ([128], [64, 64])[h]:
+                judge(bank, at - lo, "SMb", 2048 + 2048 * h + 16 * at, n, pull("OFF1", at, n, "S", 1))
+                at += n
+            H = lambda k: A("dec", 16 * k + 8 * h, 16 * k + 8 * h + 8)
+            tag[0] = "dec%d" % h
+            tt(A("CM1", lo, hi), A(bank, 0, 128), A("VJ1", lo, hi), O.is_gt)
+            wrap(96, "CM1", 0, 8 * h, 8 * h + 8)
+            tt(A("CMB", lo, hi), A("P0", lo, hi), A("CM1", lo, hi), O.max)
+            mms([(A(fb, 256, 384), A("r15", 0, 128, 1, slice(0, 1)), ONEh, True, False),
+                 (A(fb, 256, 384), A("BID"), A("CMB", lo, hi), False, True),
+                 (A(fb, 384, 512), A("ONE", 0, 128, 1, slice(0, 1)), ONEh, True, False),
+                 (A(fb, 384, 512), A("NSH"), A("CMB", lo, hi), False, True)])
+            E1 = A("P6", 96 + 8 * h, 104 + 8 * h)
+            j = 16 * (13 + h)
+            d13, d14 = A("dec", j, j + 8), A("dec", j + 8, j + 16)
+            tt(H(12), E1, H(0), O.is_ge)
+            tt(d14, E1, H(8), O.add)
+            tt(d13, H(12), H(6), O.mult)
+            tt(d14, d14, H(12), O.mult)
+            tt(d13, d13, H(5), O.add)
+            tt(d14, d14, H(7), O.add)
+            cp(A("IDX", 16 * h, 16 * h + 16), A("dec", j, j + 16))
+            iu, iv = A("IDX", 16 * h, 16 * h + 8), A("IDX", 16 * h + 8, 16 * h + 16)
+            U = sub(newl[t][0], lo, hi)
+            act(U, IND(win, iu))
+            act(A("SMg", lo, hi), IND(A("SMb", 4096 * h, 4096 * h + 4096), iv))
+            mm(A("P7", 256 + lo, 256 + hi), A("BM"), A("SMg", lo, hi), True, True)
+            tt(A("Ys", lo, hi), A(fb, 256, 384), sub(lead[t][0], lo, hi), O.mult)
+            mm(A("P6", 256 + lo, 256 + hi), A("R15"), A("Ys", lo, hi), True, True)
+            act(A("PS%d" % t, lo, hi), A("P6", 256 + lo, 256 + hi))
+            tt(A(XS, lo, hi), A(fb, 384, 512), A("BW", Sblk[t] + lo, Sblk[t] + hi), O.mult)
+            act(A("VN", lo, hi), A("P7", 256 + lo, 256 + hi))
+            tag[0] = "sc%d" % h
+            cp(IND(win, iu), A(XS, lo, hi))
+            cp(IND(A("VW", wa, we), iu), A("VN", lo, hi))
+            if h == 1:
+                send(nxt, A("PL%d" % t), A("PS%d" % t), "rp%d" % t)
+                tt(DC(12), DC(12), DC(10), O.mult)
+                tt(A(XS, 256, 272), DC(9), DC(12), O.subtract)
+                send(q, A("XL%d" % t), A(XS), "rx%d" % t)
+            tag[0] = "ol%d" % h
+            quarter(A("DIo", lo, hi), U)
+            look(A("OFFO", lo, hi), A("DIo", lo, hi), U, A("JC", 256 * t + lo, 256 * t + hi), 3)
+            for a in (lo, lo + 64) if t + 1 == RO else (lo,):
+                n = 64 if t + 1 == RO else 128
+                worth("OFFO", a, sub(newl[t][1], a, a + n), a, n, "V" if t + 1 == RO and a % 128 else "S")
+
+    recv(A("PL%d" % (RO - 1)), "rp%d" % (RO - 1), prv)
+    host_change(RO - 1)
+    fb = {0: newl[0][0], 1: newl[1][0], 2: newl[2][0], 3: ("BW", 1792)}
+    fv = {0: newl[0][1], 1: newl[1][1], 2: newl[2][1], 3: ("VW", 1792)}
+    tag[0] = "out"
+    ts(A("PO"), A("PL%d" % (RO - 1)), -296.0, O.add, -1.0, O.max)
+    dma("Y", (T.yp[:], None, 0, 0), (T.PO[15::16, :], "PO", 0, 256))
+    for s in range(4):
+        ts(A("OUT", s, 1021 + s, 4), sub(fb[s], 0, 256), -296.0, O.add, -1.0, O.max)
+        act(A("OUTV", s, 1021 + s, 4), sub(fv[s], 0, 256))
+    dma("Y", (T.yb[:], None, 0, 0), A("OUT"))
+    dma("Y", (T.yv[:], None, 0, 0), (T.OUTV[0::16, :], "OUTV", 0, 1024))
+
+    if not _order:
+        _order["o"] = arrange(ops, needs(ops))
+    for i in _order["o"]:
+        issue(ops[i])
+    for s in sorted(cnt):
+        if cnt[s]:
+            g.wait_ge(T.sem[s], cnt[s])

@@ -1,8 +1,11 @@
 from concourse.mybir import AluOpType as O, ActivationFunctionType as F
 
 RO = 3
-f32, b16, i32, u16 = "float32", "bfloat16", "int32", "uint16"
+f32, b16, f16, i32, u16 = "float32", "bfloat16", "float16", "int32", "uint16"
 SCRATCH = {}
+CH = 64
+NG = 10
+HW = 6144
 
 
 def _b(name, cols, dtype, where="sbuf"):
@@ -12,70 +15,99 @@ def _b(name, cols, dtype, where="sbuf"):
 for _k in range(8):
     _b("P%d" % _k, 512, f32, "psum")
 for _n, _c, _d in [
-    ("bunI", 1024, i32), ("potI", 256, i32), ("TB", 2064, b16), ("JC", 1024, f32), ("R01", 2048, b16),
+    ("bunI", 1024, i32), ("potI", 256, i32), ("R01", 16 * CH, b16), ("IX", 256, b16),
     ("ip", 128, i32), ("ic", 128, i32), ("id0", 128, i32), ("q1", 128, i32), ("q2", 128, i32), ("q3", 128, i32),
-    ("BM", 128, b16), ("BMq", 128, b16), ("BM8", 128, b16), ("DW", 128, b16), ("WX", 2048, b16), ("ONE", 256, b16),
-    ("cr", 512, b16), ("zr", 128, b16), ("r15", 128, b16), ("thb", 256, b16), ("THR", 256, f32),
-    ("SEL0", 128, f32), ("SEL1", 128, f32), ("SEL2", 128, f32), ("R15", 128, f32), ("NSH", 128, b16), ("BID", 128, b16),
-    ("k1", 128, b16), ("k2", 128, b16), ("rmask", 8, f32), ("wk", 16, i32), ("I1", 16, f32), ("I16", 16, f32), ("I8", 16, f32),
-    ("L0", 256, f32), ("V0L", 256, f32), ("BW", 12 * 256, f32), ("VW", 12 * 256, f32),
-    ("UB1", 512, f32), ("VB1", 512, f32), ("UB2", 256, f32), ("VB2", 256, f32),
-    ("P0in", 256, f32), ("Bz", 256, f32), ("DI", 256, i32), ("DIo", 256, i32), ("HB", 768, b16), ("Lf", 48, f32),
-    ("LV", 32, u16), ("p01", 32, f32), ("EB", 6528, b16), ("D8", 512, b16), ("D01", 512, b16),
-    ("VJ0", 256, f32), ("VJ1", 256, f32), ("VJ2", 256, f32), ("SMb", 8192, b16), ("SM2", 4096, b16), ("SMo", 4096, b16),
-    ("CM0", 512, b16), ("CM1", 256, b16), ("CMB", 256, b16), ("E02", 32, f32),
-    ("dec", 512, f32), ("IDX", 32, u16), ("Ys", 256, f32), ("SMg", 256, b16), ("VN", 256, f32), ("SMg2", 256, b16), ("VN2", 256, f32),
-    ("X2i", 32, u16), ("OFFO", 256, u16), ("OFFI", 1024, u16), ("OUT", 1024, f32), ("OUTV", 1024, f32), ("PO", 256, f32),
+    ("BM", 128, b16), ("BMn", 128, b16), ("BM8", 128, b16), ("WX", 2048, b16), ("TRI", 2048, b16), ("ONE", 16, b16), ("ZR", 16, b16),
+    ("KJ", 512, b16), ("cls", 3, f32), ("G8", 8, b16), ("G8f", 8, f16), ("LT", 16, f32),
+    ("SEL", 384, f16), ("R15", 128, f16), ("LM", 256, f32), ("NSH", 128, b16), ("BID", 128, b16),
+    ("k1", 128, b16), ("k2", 128, b16), ("col", 8, f32), ("wk", 40, i32), ("I1", 32, f32), ("PAYc", 48, f32),
+    ("L0", 256, f32), ("C3", 256, f32), ("V0", 256, b16), ("V3", 256, b16), ("BW", 2560, f32), ("VM", 2560, b16),
+    ("C1b", 256, f32), ("V1b", 256, b16), ("Bz", 256, f32), ("DS", 256, f32), ("DO", 512, f32),
+    ("HH", 256, f16), ("HB", 768, b16), ("Lf", 48, f32), ("LV", 48, u16), ("PAY", 48, f32), ("EB", 3 * 4096, b16), ("VJ", 768, b16),
+    ("SM0", HW, b16), ("SM1", HW, b16), ("SMo", 8192, b16), ("CM", 768, b16), ("KS", 64, f32), ("K1", 32, f32), ("KB", 48, i32),
+    ("IDX", 32, u16), ("Ys", 256, f32), ("XS", 256, f32), ("SMg", 256, b16),
+    ("OFFO", 256, u16), ("OFFI", 1024, u16), ("OFF", 768, u16), ("OUT", 1024, f32), ("OUTV", 1024, f32), ("PO", 256, f32),
+    ("GR", NG * 16 * CH, b16), ("h1", 1024, i32), ("h2", 256, i32),
 ]:
     _b(_n, _c, _d)
-_b("GR", 4 * 4096, b16)
-for _k in range(4):
-    _b("h1_%d" % _k, 256, i32)
-for _k in range(3):
-    _b("h2_%d" % _k, 256, i32)
-for _k in range(2):
-    _b("OFF%d" % _k, 256, u16)
+for _k in range(RO + 1):
+    _b("TB%d" % _k, 2064, b16)
 for _k in range(RO):
-    _b("OS%d" % _k, 272, u16)
-    _b("OL%d" % _k, 272, u16)
-    _b("CS%d" % _k, 256, f32)
-    _b("KS%d" % _k, 256, b16)
-    _b("KL%d" % _k, 256, b16)
-    _b("XS%d" % _k, 288, f32)
-    _b("XL%d" % _k, 288, f32)
-    _b("PS%d" % _k, 256, f32)
-    _b("PL%d" % _k, 256, f32)
-SEMAPHORES = ["v", "s", "t", "gp", "ls"] + ["d%d" % k for k in range(10)] + ["%s%d" % (n, k) for n in ("ro", "rc", "rk", "rx", "rp") for k in range(RO)]
-CP = {"cy": 1.0e-3, "pe": 0.75e-3, "gat": 1.5, "sca": 3.5, "rem": 3.2, "lat": 0.15}
-BOOST = {'g0': 16.1, 'rk': 6.3, 'rp': 4.0, 'dd1': -2.3, 'ol0': 12.0, 'ol1': 19.3, 'io': 11.4, 'rx': 19.1, 'g2': 18.4, 'j11': 2.3, 'vj2': 13.6, 'rc': -7.1, 'cs': 7.4, 'ro': 6.3, 'dec0': 0.4, 'dd2': -1.0, 'const': -6.2, 'c0': 2.7, 'look0': 6.8, 'sc1': 9.8, 'j2': -1.1, 'dec1': -0.3, 'out': 1.6, 'init': 1.3, 'vj1': 4.3, 'look1': 0.6, 'own': 0.6, 'j10': 2.0, 'hc': -2.2}
+    _b("UB%d" % _k, 256, f32)
+    _b("VU%d" % _k, 256, b16)
+    _b("PS%d" % _k, 256, f16)
+    _b("PL%d" % _k, 256, f16)
+SEMAPHORES = ["v", "s", "t", "gp", "ls", "rh"] + ["d%d" % k for k in range(12)] + ["%s%d" % (n, k) for n in ("rt", "rb", "rv", "bb", "bv", "rp", "rq") for k in range(RO)]
+CP = {"cy": 0.9e-3, "pe": 0.6e-3, "gat": 1.5, "sca": 3.5, "rem": 4.5, "tab": 14.0, "lat": 0.15, "look": 0.05, "bias": 0.5}
+BOOST = {"io": -50, "const": 60, "rt": 5, "init0": -20, "init0g": -20, "init0s": -20, "init1": -10, "init1g": 2, "init1s": 6, "init3": -8, "init3g": 1,
+         "init3s": 4, "init2": 5, "init2g": 11.5, "init2s": 12, "pool": 0, "hash0": 0, "hash1": 2, "look00": 1, "look10": 3, "look20": 5, "look01": 7,
+         "look11": 8, "look21": 9, "list": 3.5, "dd0": 6, "dd1": 6.2, "dd2": 6.4, "vj0": 9, "vj1": 9.2, "vj2": 12.2, "j00g": 10, "j10g": 11, "j20g": 12,
+         "j01g": 20, "j11g": 21, "j21g": 22, "j00s": 5.5, "j10s": 10, "j20s": 12.1, "j01s": 20.5, "j11s": 21.5, "j21s": 22.5, "dec0": 13, "ys0": 14,
+         "sc0": 14.5, "own0": 15, "own0g": 90, "own0s": 104, "dec1": 30, "ys1": 30.5, "sc1": 32, "own1": 33, "own1g": 95, "own1s": 104.5,
+         "rp": 31, "bb": 40, "rb": 105, "out": 150}
+BOOST.update({'init1s': -1.1, 'init3g': -5.4, 'init3s': 18.4, 'pool': -4.0, 'hash1': 1.0, 'look00': 2.2, 'look20': 4.7, 'look01': 9.1, 'look11': 3.6, 'dd2': 0.8, 'j10g': 8.2, 'j20g': 12.3, 'j00s': 4.8, 'j10s': 7.3, 'j11s': 18.7, 'j21s': 30.8, 'ys0': 13.4, 'own0g': 86.2, 'own0s': 101.8, 'dec1': 35.2, 'own1': 28.8, 'own1s': 106.9, 'bb': 32.6})
+BYV = [12, 15, 20, 29, 40, 49, 57, 62]
 _order = {}
 
 
+def clash(w, w2):
+    return (w or w2) and not (w == 2 and w2 == 2)
+
+
 def needs(ops):
-    n = len(ops)
-    dep = [set() for _ in range(n)]
+    dep = [set() for _ in ops]
     hist = {}
     for i, o in enumerate(ops):
-        if o["after"] is not None:
-            dep[i].add(o["after"])
-        for lst, w in ((o["ins"], False), (o["outs"], True)):
-            for x in lst:
-                nm, lo, hi = x[1], x[2], x[3]
-                if nm is None:
-                    continue
-                ps = SCRATCH[nm][0] == "psum" if nm in SCRATCH else False
-                for (l, h, w2, k) in hist.get(nm, ()):
-                    if k != i and ((w or w2) and l < hi and h > lo or ps and ops[k]["q"] != o["q"]):
-                        dep[i].add(k)
-        for lst, w in ((o["ins"], False), (o["outs"], True)):
-            for x in lst:
-                nm, lo, hi = x[1], x[2], x[3]
-                if nm is None:
-                    continue
-                if w:
-                    hist[nm] = [r for r in hist.get(nm, []) if not (r[0] >= lo and r[1] <= hi)]
-                hist.setdefault(nm, []).append((lo, hi, w, i))
+        dep[i].update(o["after"])
+        for x, w in o["use"]:
+            for (l, h, w2, k) in hist.get(x[1], ()):
+                if k != i and clash(w, w2) and l < x[3] and h > x[2]:
+                    dep[i].add(k)
+        for x, w in o["use"]:
+            if w == 1:
+                hist[x[1]] = [r for r in hist.get(x[1], []) if not (r[0] >= x[2] and r[1] <= x[3])]
+            hist.setdefault(x[1], []).append((x[2], x[3], w, i))
     return dep
+
+
+def lay(ops, dep, suc, pr, fwd):
+    n = len(ops)
+    left = [len(d) for d in dep]
+    rdy = [0.0] * n
+    at = [0.0] * n
+    free = {}
+    bank = {}
+    pool = [i for i in range(n) if not left[i]]
+    order = []
+
+    def when(i, q):
+        return max([rdy[i]] + [bank[b][0] for b in ops[i]["banks"] if b in bank and bank[b][1] != q])
+
+    while pool:
+        best = None
+        for q in "RYGTSV":
+            c = [(when(i, q), i) for i in pool if q in ops[i]["var"]]
+            if not c:
+                continue
+            t = max(free.get(q, 0.0), min(c)[0])
+            if best is None or t < best[0]:
+                w, k = max((x for x in c if x[0] <= t + CP["look"]),
+                           key=lambda x: pr[x[1]] - (CP["bias"] if q == "V" and len(ops[x[1]]["var"]) > 1 else 0.0))
+                best = (t, q, k, max(t, w))
+        _, q, i, t = best
+        pool.remove(i)
+        order.append((i, q))
+        end = t + ops[i]["var"][q][1]
+        at[i] = end
+        free[q] = end if q != "R" else 0.0
+        for b in ops[i]["banks"]:
+            bank[b] = (end + CP["lat"], q)
+        for k in suc[i]:
+            rdy[k] = max(rdy[k], end + ops[i if fwd else k]["lat"])
+            left[k] -= 1
+            if not left[k]:
+                pool.append(k)
+    return order, at, max(at[i] + ops[i]["lat"] for i in range(n))
 
 
 def arrange(ops, dep):
@@ -86,57 +118,57 @@ def arrange(ops, dep):
             suc[k].append(i)
     pr = [0.0] * n
     for i in range(n - 1, -1, -1):
-        pr[i] = ops[i]["cost"] + ops[i]["lat"] + max([pr[k] for k in suc[i]] + [0.0]) + BOOST.get(ops[i]["tag"], 0.0)
-    left = [len(d) for d in dep]
-    rdy = [0.0] * n
-    free = {}
-    pool = {}
-    for i in range(n):
-        if not left[i]:
-            pool.setdefault(ops[i]["q"], []).append(i)
-    order = []
-    while len(order) < n:
-        best = None
-        for q, c in pool.items():
-            if not c:
-                continue
-            f = free.get(q, 0.0)
-            t = max(f, min(rdy[i] for i in c))
-            if best is None or t < best[0]:
-                k = max((i for i in c if rdy[i] <= t + 1e-9), key=lambda i: pr[i])
-                best = (t, q, k)
-        t, q, i = best
-        pool[q].remove(i)
-        order.append(i)
-        end = t + ops[i]["cost"]
-        free[q] = end if q != "R" else 0.0
-        for k in suc[i]:
-            rdy[k] = max(rdy[k], end + ops[i]["lat"])
-            left[k] -= 1
-            if not left[k]:
-                pool.setdefault(ops[k]["q"], []).append(k)
-    return order
+        pr[i] = max([-100.0 * ops[i]["round"] - BOOST[ops[i]["tag"]]] + [pr[k] for k in suc[i]]) + 1e-3
+    return lay(ops, dep, suc, pr, True)[0]
 
 
 def rank_program(g, core, T, topo):
+    N = len(T.cores)
+
+    def helper(c):
+        return [x for x in topo.cores_of(c) if topo.die(x) != topo.die(c)][0]
+
+    def inner(c):
+        far = [topo.engines(c, x) for x in T.cores if x != c]
+        return [e for e in topo.engines(c, helper(c)) if not any(e in f for f in far)]
+
     rank = T.rank_of(core)
     if rank is None:
+        for r, c in enumerate(T.cores):
+            if helper(c) == core:
+                g.wait_ge(T.sem.rh, len(inner(c)))
+                out = 0
+                for t in range(1, RO):
+                    dst = T.cores[(r - 1 - t) % N]
+                    rid, pid = topo.addr(dst, core)
+                    g.remote_dma(T["TB%d" % (t + 1)][:], T.TB0[:], T.sem["rt%d" % t], T.sem.ls, pid, rid, topo.mask(core, dst))
+                    out += len(topo.engines(core, dst))
+                g.wait_ge(T.sem.ls, out)
         return
-    N = len(T.cores)
     eng = {"V": g.vector, "S": g.scalar, "T": g.tensor, "Y": g.sync, "G": g}
     own = {"V": "v", "S": "s", "T": "t", "G": "gp"}
     cnt = {"v": 0, "s": 0, "t": 0, "gp": 0, "ls": 0}
     know = {q: {} for q in eng}
     recs = {}
     nd = [0]
-    tag = [""]
+    ring = [0, 0]
+    tag = ["", 0]
     ops = []
     sent = {}
+    todo = {}
+    begun = set()
+    cy = CP["cy"]
 
     def A(n, lo=0, hi=None, st=1, ps=slice(None)):
         if hi is None:
             hi = T[n].shape[1]
         return (T[n][ps, lo:hi:st], n, lo, hi)
+
+    def sub(x, lo, hi):
+        return A(x[0], x[1] + lo, x[1] + hi)
+
+    def hbm(ap):
+        return (ap, None, 0, 0)
 
     def cols(x):
         return x[0].shape[1]
@@ -144,110 +176,117 @@ def rank_program(g, core, T, topo):
     def IND(w, o):
         return (w[0].indirect(o[0]), [w, o])
 
-    def flat(lst):
-        out = []
-        for o in lst:
-            if isinstance(o[1], list):
-                out += o[1]
-            else:
-                out.append(o)
-        return out
-
-    def add(q, fns, outs, ins, cost, lat=None, after=None, kind="c"):
-        ops.append({"q": q, "fns": fns, "outs": flat(outs), "ins": flat(ins), "cost": cost, "lat": CP["lat"] if lat is None else lat,
-                    "after": after, "kind": kind, "tag": tag[0]})
-
-    def two(x):
-        return SCRATCH[x[1]][2] in (b16, u16)
+    def ind(x):
+        return isinstance(x[1], list)
 
     def psum(x):
-        return SCRATCH[x[1]][0] == "psum"
+        return x[1] in SCRATCH and SCRATCH[x[1]][0] == "psum"
+
+    def two(x):
+        return SCRATCH[x[1]][2] in (b16, f16, u16)
+
+    def add(var, outs, ins, lat=None, after=(), kind="c", more=()):
+        use = list(more)
+        for lst, w in ((ins, 0), (outs, 1)):
+            for x in lst:
+                if ind(x):
+                    use += [(x[1][0], w), (x[1][1], 0)]
+                elif x[1] is not None:
+                    use.append((x, w))
+        ops.append({"var": var, "use": use, "lat": CP["lat"] if lat is None else lat, "after": list(after), "kind": kind, "tag": tag[0], "round": tag[1],
+                    "banks": sorted(set(x[1] for x, w in use if psum(x)))})
+
+    def plain(o, a):
+        return max(64, cols(a) * (0.5 if two(o) and two(a) else 1)) * cy
 
     def tt(o, a, b, op):
-        if isinstance(a[1], list):
-            c = 0.06 + 16 * cols(a[1][1]) * CP["gat"] * CP["cy"]
-        else:
-            c = max(64, cols(a) * (1 if psum(a) or psum(b) else 2)) * CP["cy"]
-        add("V", [lambda: g.vector.tensor_tensor(o[0], a[0], b[0], op)], [o], [a, b], c)
+        c = max(64, cols(a) * (1 if psum(a) or psum(b) else 2)) * cy
+        add({"V": ([lambda: g.vector.tensor_tensor(o[0], a[0], b[0], op)], c)}, [o], [a, b])
+
+    def vts(o, a, s1, op0, s2=None, op1=None):
+        v1 = s1[0] if isinstance(s1, tuple) else s1
+        if op1 is None:
+            return [lambda: g.vector.tensor_scalar(o[0], a[0], v1, None, op0)], plain(o, a)
+        return [lambda: g.vector.tensor_scalar(o[0], a[0], v1, s2, op0, op1)], plain(o, a)
 
     def ts(o, a, s1, op0, s2=None, op1=None):
-        x = [a] + [s for s in (s1,) if isinstance(s, tuple)]
-        v1 = s1[0] if isinstance(s1, tuple) else s1
-        c = max(64, cols(a) * (0.5 if two(o) and two(a) else 1)) * CP["cy"]
-        if op1 is None:
-            add("V", [lambda: g.vector.tensor_scalar(o[0], a[0], v1, None, op0)], [o], x, c)
-        else:
-            add("V", [lambda: g.vector.tensor_scalar(o[0], a[0], v1, s2, op0, op1)], [o], x, c)
+        add({"V": vts(o, a, s1, op0, s2, op1)}, [o], [a] + ([s1] if isinstance(s1, tuple) else []))
 
     def cp(o, a):
-        if isinstance(o[1], list):
-            c = 0.06 + 16 * cols(o[1][1]) * CP["sca"] * CP["cy"]
-        elif isinstance(a[1], list):
-            c = 0.06 + 16 * cols(a[1][1]) * CP["gat"] * CP["cy"]
-        else:
-            c = max(64, cols(a) * (0.5 if two(o) and two(a) else 1)) * CP["cy"]
-        add("V", [lambda: g.vector.tensor_copy(o[0], a[0])], [o], [a], c)
+        c = 0.06 + 16 * cols(o[1][1]) * CP["sca"] * cy if ind(o) else plain(o, a)
+        add({"V": ([lambda: g.vector.tensor_copy(o[0], a[0])], c)}, [o], [a])
 
     def fill(o, c):
-        add("V", [lambda: g.vector.memset(o[0], c)], [o], [], max(64, cols(o) * (0.5 if two(o) else 1)) * CP["cy"])
+        add({"V": ([lambda: g.vector.memset(o[0], c)], plain(o, o))}, [o], [])
 
-    def act(o, a, scale=1.0):
-        c = 0.07 + 16 * cols(a[1][1]) * CP["gat"] * CP["cy"] if isinstance(a[1], list) else 0.1 + cols(a) * CP["cy"]
-        if isinstance(scale, tuple):
-            add("S", [lambda: g.scalar.activation(o[0], a[0], F.Copy, 0.0, scale[0])], [o], [a, scale], c)
-        else:
-            add("S", [lambda: g.scalar.activation(o[0], a[0], F.Copy)], [o], [a], c)
+    def move(o, a):
+        c = 0.06 + 16 * cols(a[1][1]) * CP["gat"] * cy if ind(a) else None
+        add({"V": ([lambda: g.vector.tensor_copy(o[0], a[0])], c or plain(o, a)),
+             "S": ([lambda: g.scalar.activation(o[0], a[0], F.Copy)], c or max(64, cols(a)) * cy)}, [o], [a])
 
-    def mms(lst):
+    def lin(o, a, m, c):
+        add({"V": vts(o, a, m, O.mult, c, O.add),
+             "S": ([lambda: g.scalar.activation(o[0], a[0], F.Identity, c, m)], max(64, cols(a)) * cy)}, [o], [a])
+
+    def scale(o, a, m, c):
+        add({"V": vts(o, a, m, O.mult, c[0], O.add),
+             "S": ([lambda: g.scalar.activation(o[0], a[0], F.Identity, c[0], m[0])], max(64, cols(a)) * cy)}, [o], [a, m, c])
+
+    def relu(o, a, c):
+        add({"V": vts(o, a, c, O.add, 0.0, O.max),
+             "S": ([lambda: g.scalar.activation(o[0], a[0], F.Relu, c, 1.0)], max(64, cols(a)) * cy)}, [o], [a])
+
+    def mms(lst, grp=None, first=True):
+        bank = lst[0][0][1]
+        key = grp or ("g", len(ops))
+        todo[key] = todo.get(key, 0) + len(lst)
+
         def one(x):
-            return lambda: g.tensor.matmul(x[0][0], x[1][0], x[2][0], x[3], x[4])
-        c = sum(max(64, cols(x[2])) * (1 if two(x[1]) else 4) for x in lst) * CP["pe"]
-        add("T", [one(x) for x in lst], [x[0] for x in lst], [y for x in lst for y in x[1:3]], c)
-
-    def mm(o, l, r, s, e):
-        mms([(o, l, r, s, e)])
+            def f():
+                todo[key] -= 1
+                st = key not in begun
+                begun.add(key)
+                return g.tensor.matmul(x[0][0], x[1][0], x[2][0], st, todo[key] == 0)
+            return f
+        c = sum(max(min(64, cols(x[1])), cols(x[2])) * (1 if two(x[1]) else 4) for x in lst) * CP["pe"]
+        tok = (None, "grp" + bank, 0, 1)
+        more = [(tok, 1 if first else 0)] + ([] if first else [(x[0], 2) for x in lst])
+        add({"T": ([one(x) for x in lst], c)}, [x[0] for x in lst] if first else [],
+            [y for x in lst for y in x[1:3]], more=more)
 
     def iota(o, pat, base, cm):
-        c = 0.15 + 2 * cols(o) * CP["cy"]
+        c = 0.15 + 2 * cols(o) * cy
         if SCRATCH[o[1]][2] != i32:
-            add("G", [lambda: g.iota(o[0], pat, base, cm, allow_small_or_imprecise_dtypes=True)], [o], [], c)
+            add({"G": ([lambda: g.iota(o[0], pat, base, cm, allow_small_or_imprecise_dtypes=True)], c)}, [o], [])
         else:
-            add("G", [lambda: g.iota(o[0], pat, base, cm)], [o], [], c)
+            add({"G": ([lambda: g.iota(o[0], pat, base, cm)], c)}, [o], [])
 
-    def dma(q, out, in_):
-        tag[0] = "io"
-        add(q, [lambda: eng[q].dma_start(out[0], in_[0])], [out] if out[1] else [], [in_] if in_[1] else [], 0.1, 3.0, None, "d")
+    def dma(q, out, in_, lat=3.0):
+        add({q: ([lambda: eng[q].dma_start(out[0], in_[0])], 0.1)}, [out], [in_], lat, kind="d")
 
-    def send(dst, out, in_, sem):
-        m = topo.mask(core, dst)
+    def send(dst, out, in_, sem, after=()):
+        es = inner(core) if dst == helper(core) else topo.engines(core, dst)
+        m = sum(1 << e for e in es)
         rid, pid = topo.addr(dst, core)
-        cnt["ls"] += len(topo.engines(core, dst))
+        cnt["ls"] += len(es)
         sent[sem] = len(ops)
-        add("G", [lambda: g.remote_dma(out[0], in_[0], T.sem[sem], T.sem.ls, pid, rid, m)], [], [in_], 0.4, 0.0, None, "r")
-        ops[-1]["tag"] = sem[:2]
+        add({"G": ([lambda: g.remote_dma(out[0], in_[0], T.sem[sem], T.sem.ls, pid, rid, m)], 0.4)}, [], [in_], 0.0, after, "r")
 
-    def recv(out, sem, src):
-        ne = len(topo.engines(src, core))
-        add("R", [(sem, ne)], [out], [], 0.0, CP["rem"], sent[sem], "v")
+    def recv(out, sem, src, lat=None):
+        add({"R": ([(sem, len(topo.engines(src, core)), out)], 0.0)}, [out], [], lat or CP["rem"], [sent[sem]], "v")
 
-    def wait_for(q, outs, ins):
+    def wait_for(q, use):
         need = []
-        for lst, w in ((ins, False), (outs, True)):
-            for o in lst:
-                n, lo, hi = o[1], o[2], o[3]
-                if n is None:
+        for x, w in use:
+            n, lo, hi = x[1], x[2], x[3]
+            if n not in SCRATCH:
+                continue
+            ps = psum(x)
+            for r in recs.get(n, ()):
+                if r[3] == q and q == "T" and ps:
                     continue
-                ps = SCRATCH[n][0] == "psum" if n in SCRATCH else False
-                for r in recs.get(n, ()):
-                    if r[3] == q:
-                        if q == "T" and ps:
-                            continue
-                        if (w or r[2]) and r[0] < hi and r[1] > lo:
-                            need.append(r)
-                    elif ps:
-                        need.append(r)
-                    elif r[0] < hi and r[1] > lo and (w or r[2]):
-                        need.append(r)
+                if (ps and r[3] != q) or (r[0] < hi and r[1] > lo and (w or r[2])):
+                    need.append(r)
         kn = know[q]
         need = [r for r in need if kn.get(r[4], 0) < r[5]]
         need.sort(key=lambda r: -sum(r[6].values()))
@@ -259,386 +298,332 @@ def rank_program(g, core, T, topo):
                         kn[s] = v
 
     def note(n, lo, hi, w, q, sem, val, clk):
-        if n is None:
+        if n not in SCRATCH:
             return
-        if w:
+        if w == 1:
             recs[n] = [r for r in recs.get(n, []) if not (r[0] >= lo and r[1] <= hi)]
         recs.setdefault(n, []).append((lo, hi, w, q, sem, val, clk))
 
-    def issue(o):
-        q = o["q"]
+    def issue(o, q):
+        fns = o["var"][q][0]
         if o["kind"] == "v":
-            sem, ne = o["fns"][0]
+            sem, ne, x = fns[0]
             cnt[sem] = ne
-            x = o["outs"][0]
-            note(x[1], x[2], x[3], True, "R", sem, ne, {sem: ne})
+            note(x[1], x[2], x[3], 1, "R", sem, ne, {sem: ne})
             return
-        wait_for(q, o["outs"], o["ins"])
+        wait_for(q, o["use"])
         if o["kind"] == "r":
-            o["fns"][0]()
+            fns[0]()
             return
         if o["kind"] == "d":
             s, by = "d%d" % nd[0], "D"
             nd[0] += 1
             cnt[s] = 16
-            o["fns"][0]().then_inc(T.sem[s], 16)
+            fns[0]().then_inc(T.sem[s], 16)
         else:
             s, by = own[q], q
-            for f in o["fns"]:
+            for f in fns:
                 cnt[s] += 1
                 f().then_inc(T.sem[s], 1)
         clk = dict(know[q])
         clk[s] = cnt[s]
-        for x in o["ins"]:
-            note(x[1], x[2], x[3], False, by, s, cnt[s], clk)
-        for x in o["outs"]:
-            note(x[1], x[2], x[3], True, by, s, cnt[s], clk)
+        for x, w in o["use"]:
+            note(x[1], x[2], x[3], w, by, s, cnt[s], clk)
 
-    def pull(off, lo, n, q="S", kind=0, at=None):
-        k = 4096 * kind + 16 * (lo if at is None else at)
-        o, w = A("GR", k, k + 16 * n), IND(A("TB"), A(off, lo, lo + n))
-        if q == "S":
-            act(o, w)
-        else:
-            cp(o, w)
-        return k
+    def sights(tab, off, lo, dst, first, step):
+        k = 16 * CH * (ring[0] % NG)
+        ring[0] += 1
+        n = 16 * CH
+        move(A("GR", k, k + n), IND(A(tab), A(off, lo, lo + CH)))
+        del ops[-1]["var"]["S" if ring[0] - 1 in BYV else "V"]
+        ops[-1]["tag"] += "g"
+        e = first + step * (n - 1)
+        o = (T[dst][:, e:(first - step if first >= step else None):-step], dst, first, e + 1)
+        d = (T.GR[:, k + n - 1:(k - 1 if k else None):-1], "GR", k, k + n)
+        z = A("R01")
+        add({"V": ([lambda: g.vector.tensor_tensor_scan(o[0], z[0], d[0], 0.0, O.min, O.max)], n / 2 * cy)}, [o], [z, d])
+        ops[-1]["tag"] += "s"
 
-    def scan(n, lo, k, m):
-        e = lo + 16 * m
-        o = (T[n][:, e - 1:(lo - 1 if lo else None):-1], n, lo, e)
-        d = (T.GR[:, k + 16 * m - 1:(k - 1 if k else None):-1], "GR", k, k + 16 * m)
-        z = (T.R01[:, 16 * m - 1::-1], "R01", 0, 16 * m)
-        add("V", [lambda: g.vector.tensor_tensor_scan(o[0], z[0], d[0], 0.0, O.mult, O.max)], [o], [z, d], 8 * m * CP["cy"])
+    def W(y):
+        return A("WX", 128 * y, 128 * y + 128)
 
-    dma("Y", A("bunI"), (T.bun[:], None, 0, 0))
-    dma("S", A("TB", 37, 2048), (T.sight[:, 0:2011], None, 0, 0))
-    dma("S", A("TB", 0, 37), (T.sight[:, 2011:2048], None, 0, 0))
+    def back(k):
+        return T.cores[(rank - k) % N]
+
+    def ahead(k):
+        return T.cores[(rank + k) % N]
+
+    tag[0] = "io"
+    dma("Y", A("bunI", 0, 512), hbm(T.bun[:, 0:512]), 4.5)
+    dma("S", A("TB0", 37, 2048), hbm(T.sight[:, 0:2011]), 4.0)
+    dma("S", A("TB0", 0, 37), hbm(T.sight[:, 2011:2048]), 4.0)
+    dma("Y", A("bunI", 512, 1024), hbm(T.bun[:, 512:1024]), 6.0)
     fill(A("potI"), -1)
-    dma("Y", (T.potI[15::16, :], "potI", 0, 256), (T.pots[:], None, 0, 0))
-    iota(A("JC"), [[1, 4], [4, 256]], 1, 0)
+    dma("Y", (T.potI[15::16, :], "potI", 0, 256), hbm(T.pots[:]), 6.0)
     iota(A("ip"), [[0, 128]], 0, 1)
     iota(A("ic"), [[1, 128]], 0, 0)
     iota(A("id0"), [[-1, 128]], 0, 1)
-    iota(A("wk"), [[16, 16]], 0, 0)
-    tag[0] = "const"
-    fill(A("TB", 2048, 2064), 0.0)
-    fill(A("R01"), 1.0)
-    fill(A("R01", 15, 2048, 16), 0.0)
-    fill(A("ONE"), 1.0)
-    fill(A("WX"), 0.0)
-    for y in range(16):
-        fill(A("thb", y, 256, 16), 2.0 ** -y)
+    iota(A("wk", 0, 16), [[0, 2], [16, 8]], 0, 0)
+    iota(A("wk", 16, 32), [[16, 16]], 0, 0)
+    iota(A("wk", 32, 35), [[1, 3]], 1, 1)
+    iota(A("IX", 0, 256, 1, slice(0, 2)), [[1, 256]], 0, 1)
     for s in range(4):
-        fill(A("cr", 128 * s, 128 * s + 128), float(s + 1))
-    fill(A("zr"), 0.0)
-    fill(A("r15"), 0.0)
-    fill(A("r15", 15, 128, 16), 1.0)
+        iota(A("KJ", 128 * s, 128 * s + 128, 1, slice(0, 2)), [[0, 128]], 3 - s, 2 * s - 2)
+    iota(A("R01"), [[0, CH], [256, 16]], 0, 0)
+    tag[0] = "const"
+    fill(A("TB0", 2048, 2064), 0.0)
+    fill(A("ONE"), 1.0)
+    fill(A("ZR"), 0.0)
+    ts(A("wk", 32, 35), A("wk", 32, 35), 3, O.bitwise_and)
+    ts(A("cls"), A("wk", 32, 35), 1.0, O.add, 0.25, O.mult)
+    fill(A("WX"), 0.0)
+    fill(A("CM"), 0.0)
+    for t in range(RO):
+        fill(A("VM", 768 * t + 512, 768 * t + 768), 0.0)
     ts(A("q1"), A("ip"), 4, O.arith_shift_right)
     ts(A("q2"), A("ic"), 4, O.arith_shift_right)
     tt(A("BM"), A("q1"), A("q2"), O.is_equal)
     ts(A("q3"), A("ip"), 15, O.bitwise_and)
     for gg in range(8):
         ts(A("WX", 16 * gg, 16 * gg + 15 * 129 + 1, 129), A("ONE", 0, 16), A("BM", 16 * gg, 16 * gg + 1), O.mult)
-
-    def W(y):
-        return A("WX", 128 * y, 128 * y + 128)
-
-    ts(A("BMq"), A("BM"), 0.25, O.mult)
-    ts(A("BM8"), A("BM"), 8.0, O.mult)
+    ts(A("BMn"), A("BM"), -1.0, O.mult)
+    ts(A("BM8"), A("BM"), -8192.0, O.mult)
+    cp(A("G8"), A("BM", 0, 128, 16))
+    cp(A("G8f"), A("BM", 0, 128, 16))
     for m in range(3):
-        ts(A("k1"), A("q3"), m, O.is_equal)
-        tt(A("SEL%d" % m), A("k1"), A("BM"), O.mult)
-    ts(A("rmask", 0, 1), A("q3", 0, 1), 15, O.not_equal)
+        ts(A("col", m, m + 1), A("q3", 0, 1), m, O.is_equal, 4.0, O.mult)
+        ts(A("SEL", 128 * m, 128 * m + 128), A("BM"), A("col", m, m + 1), O.mult)
+    tt(A("LT"), A("q3", 0, 16), A("ic", 0, 16), O.is_lt)
+    for x in range(1, 16):
+        ts(A("TRI", 128 * x, 128 * x + 128), A("BM8"), A("LT", x, x + 1), O.mult)
     cp(A("R15"), W(15))
+    fill(A("col", 3, 4), 0.0)
+    ts(A("col", 4, 5), A("q3", 0, 1), 15, O.not_equal)
+    ts(A("col", 6, 7), A("col", 4, 5), -1.0, O.add)
+    ts(A("col", 7, 8), A("col", 6, 7), -2344.0, O.mult)
     ts(A("k1"), A("id0"), 1, O.is_equal)
     tt(A("k1"), A("k1"), A("BM"), O.mult)
-    ts(A("NSH"), A("k1"), -1.0, O.mult)
-    ts(A("k2"), A("id0"), 2, O.is_equal)
+    ts(A("NSH"), A("k1"), -0.625, O.mult)
+    ts(A("k2"), A("id0"), 2, O.is_equal, 4.0, O.mult)
     tt(A("k2"), A("k2"), A("BM"), O.mult)
     tt(A("k1"), A("k1"), A("k2"), O.subtract)
-    ts(A("k2"), A("q3"), 1, O.is_equal)
-    tt(A("k2"), A("k2"), W(15), O.mult)
-    tt(A("BID"), A("k1"), A("k2"), O.subtract)
-    tt(A("I1"), A("q3", 0, 16), A("wk"), O.add)
-    ts(A("I16"), A("I1"), 16.0, O.mult)
-    for h in range(2):
-        cp(A("I8", 8 * h, 8 * h + 8), A("I16", 0, 8))
-    ts(A("THR"), A("thb"), 2.0, O.mult)
-    mm(A("P4", 0, 128), A("thb", 0, 128, 1, slice(0, 1)), A("ONE", 0, 128, 1, slice(0, 1)), True, True)
-    tt(A("DW"), A("P4", 0, 128), A("BM"), O.mult)
-    ONE1 = A("ONE", 0, 256, 1, slice(0, 1))
-    ONEh = A("ONE", 0, 128, 1, slice(0, 1))
-    iota(A("BW", 1536, 1792), [[0, 256]], 0, 0)
-    iota(A("BW", 2304, 2560), [[0, 256]], 0, 0)
+    ts(A("col", 5, 6), A("q3", 0, 1), 1, O.is_equal)
+    ts(A("k2"), W(15), A("col", 5, 6), O.mult)
+    tt(A("k1"), A("k1"), A("k2"), O.subtract)
+    ts(A("BID"), A("k1"), 2.0, O.mult)
+    tt(A("I1"), A("q3", 0, 32), A("wk", 0, 32), O.add)
+    slot = [0, 768, 256, 512]
+    for m in range(3):
+        ts(A("PAYc", 16 * m, 16 * m + 16), A("I1", 0, 16), 131072.0, O.mult, 2048.0 * (2 - m) - 8192 + slot[m], O.add)
+    ts(A("KS", 48, 64), A("I1", 0, 16), 131072.0, O.mult, 4096.0 - 8192 + slot[3], O.add)
+    tt(A("KS", 48, 64), A("KS", 48, 64), A("I1", 16, 32), O.add)
 
     def goods(o, src, pt):
         ts(pt, src, 0, O.is_ge, 296.0, O.mult)
         tt(o, pt, src, O.add)
 
-    def look(o, D, c, J, k):
-        h1 = A("h1_%d" % k, 0, cols(c))
-        tt(h1, c, J, O.mult)
-        tt(h1, h1, D, O.add)
-        ts(h1, h1, 3, O.arith_shift_right, 2047 | (1 << 20), O.bitwise_and)
+    def look(o, D, c, J):
+        n = cols(c)
+        k = 256 * (ring[1] % 4)
+        ring[1] += 1
+        h1 = A("h1", k, k + n)
+        tt(J, c, J, O.mult)
+        tt(h1, J, D, O.add)
+        ts(h1, h1, 3, O.arith_shift_right, 2047 | (1 << 23), O.bitwise_and)
         ts(o, h1, 2048, O.min)
 
-    def quarter(o, c):
-        ts(o, c, 0.25, O.mult, -74.375, O.add)
+    def mine(c, s, lo, n, J, off, at, dst, sm):
+        D = A("DO", at % 512, at % 512 + n)
+        lin(D, c, 0.25, -74.5)
+        mms([(J, A("KJ", 128 * s, 128 * s + 128, 1, slice(0, 2)), A("IX", lo, lo + n, 1, slice(0, 2)))])
+        look(A(off, at, at + n), D, c, J)
+        for a in range(0, n, CH):
+            sights("TB0", off, at + a, "SMo", sm + 16 * a, 1)
+        move(dst, A("SMo", sm, sm + 16 * n, 16))
+        ops[-1]["tag"] += "s"
 
-    def worth(off, lo, dst, at, n, q="S"):
-        tag[0] = "own"
-        k = pull(off, lo, n, q, 3, at)
-        scan("SMo", 16 * at, k, n)
-        mm(A("P7", at, at + n), A("BM"), A("SMo", 16 * at, 16 * at + 16 * n, 16), True, True)
-        act(dst, A("P7", at, at + n))
-
-    BWc = {1: ("BW", 512), 2: ("BW", 768), 3: ("BW", 1792), 0: ("L0", 0)}
-    VWc = {1: ("VW", 512), 2: ("VW", 768), 3: ("VW", 1792), 0: ("V0L", 0)}
-
-    def sub(x, lo, hi):
-        return A(x[0], x[1] + lo, x[1] + hi)
-    act(A("P5"), A("JC", 0, 512))
-    act(A("P6"), A("JC", 512, 1024))
-    tag[0] = "init"
-    for s in range(4):
-        goods(sub(BWc[s], 0, 256), A("bunI", s, 1024, 4), A("P%d" % s, 0, 256))
-        quarter(A("DIo"), sub(BWc[s], 0, 256))
-        look(A("OFFI", 256 * s, 256 * s + 256), A("DIo"), sub(BWc[s], 0, 256), A("P%d" % (5 + s // 2), 256 * (s % 2), 256 * (s % 2) + 256), s)
-    goods(A("P0in"), A("potI"), A("P4", 0, 256))
+    tag[0] = "rt"
+    send(back(1), A("TB1"), A("TB0"), "rt0")
+    send(helper(core), A("TB0"), A("TB0"), "rh", [sent["rt0"]])
+    for t in range(1, RO):
+        sent["rt%d" % t] = sent["rh"]
+    first = {0: (("L0", 0), ("V0", 0)), 1: (("BW", 0), ("VM", 0)), 2: (("BW", 768), ("VM", 768)), 3: (("C3", 0), ("V3", 0))}
 
     def first_worth(s):
         for h in range(2):
-            worth("OFFI", 256 * s + 128 * h, sub(VWc[s], 128 * h, 128 * h + 128), 128 * h, 128)
+            tag[0] = "init%d" % s
+            lo = 128 * h
+            bank = "P%d" % (5 + h)
+            c = sub(first[s][0], lo, lo + 128)
+            goods(c, A("bunI", s + 4 * lo, 4 * lo + 512, 4), A(bank, 384, 512))
+            mine(c, s, lo, 128, A(bank, 256, 384), "OFFI", 256 * s + lo, sub(first[s][1], lo, lo + 128), 4096 * (s & 1) + 16 * lo)
+
     first_worth(0)
-    first_worth(1)
-
-    wins = [(0, 1024, 0, 512, 768), (768, 2048, 256, 0, 1024), (1792, 3072, 768, 0, 256)]
-    Sblk = [0, 1024, 2560]
-    hostw = [("BW", "VW", 1536, 2048, 256, 0), ("BW", "VW", 2048, 2560, 0, 256), ("UB1", "VB1", 0, 512, 0, 256)]
-    lead = [(("L0", 0), ("V0L", 0)), (("BW", 512), ("VW", 512)), (("BW", 768), ("VW", 768))]
-    newl = [(("BW", 2048), ("VW", 2048)), (("UB1", 0), ("VB1", 0)), (("UB2", 0), ("VB2", 0))]
-    nxt, prv = T.cores[(rank + 1) % N], T.cores[(rank - 1) % N]
-
-    def DC(k, w=16):
-        return A("dec", 16 * k, 16 * k + w)
-
-    def wrap(at, src, lo, k0=0, k1=16):
-        mms([(A("P6", at + k0, at + k1), W(y), A(src, lo + 16 * k0 + y, lo + 16 * k1, 16), y == 0, y == 15) for y in range(16)])
-
-    def judge(bank, at, smn, lo, n, k):
-        scan(smn, lo, k, n)
-        mms([(A(bank, at, at + n), W(d), A(smn, lo + d, lo + 16 * n, 16), d == 0, d == 15) for d in range(16)])
-
-    def dedup(m):
-        base = 2176 * m
-        o = [base + sum(256 - 16 * j for j in range(k)) for k in range(17)]
-        for k in range(16):
-            ts(A("EB", o[k], o[k + 1]), A("HB", 256 * m + 16 * k, 256 * m + 256), A("Lf", 16 * m + k, 16 * m + k + 1), O.is_equal)
-        P = "P%d" % m
-        l = [(A(P, 0, 256), A("zr", 0, 128, 1, slice(0, 1)), ONE1, True, False)]
-        for k in range(16):
-            if k < 15:
-                l.append((A(P, 16 * k + 16, 256), A("BM8"), A("EB", o[k] + 16, o[k + 1]), False, False))
-            l.append((A(P, 16 * k, 16 * k + 16), A("DW"), A("EB", o[k], o[k] + 16), False, k == 15))
-        for a in range(0, len(l), 4):
-            mms(l[a:a + 4])
-
-    def host_change(t):
-        bw, vw, a, e, cb, db = hostw[t]
-        recv(A("XL%d" % t), "rx%d" % t, T.cores[(rank - 1 - t) % N])
-        tag[0] = "hc"
-        cp(A("X2i"), A("XL%d" % t, 256, 288))
-        act(A("SMg2"), IND(A("SM2"), A("X2i", 16, 32)))
-        mm(A("P7", 256, 512), A("BM"), A("SMg2"), True, True)
-        act(A("VN2"), A("P7", 256, 512))
-        cp(IND(A(bw, a, e), A("X2i", 0, 16)), A("XL%d" % t, 0, 256))
-        cp(IND(A(vw, a, e), A("X2i", 0, 16)), A("VN2"))
+    tag[0] = "pool"
+    ts(A("P2", 256, 512), A("potI"), 0, O.is_ge, 296.0, O.mult)
+    tt(A("P7", 256, 512), A("P2", 256, 512), A("potI"), O.add)
+    home = [(("BW", 1536), ("VM", 1536)), (("BW", 2304), ("VM", 2304)), (("C1b", 0), ("V1b", 0))]
 
     for t in range(RO):
-        q, p = T.cores[(rank + 1 + t) % N], T.cores[(rank - 1 - t) % N]
-        LB, LVv = sub(lead[t][0], 0, 256), sub(lead[t][1], 0, 256)
-        wa, we, so, c0, c1 = wins[t]
-        S = A("BW", Sblk[t], Sblk[t] + 256)
-        if t == 0:
-            pool = A("P0in")
-        else:
-            pool = A("PL%d" % (t - 1))
-            recv(pool, "rp%d" % (t - 1), prv)
-        tag[0] = "hash"
-        ts(A("Bz"), LB, 39.0, O.max, 13.0 * t + 216.0, O.add)
-        act(A("P5", 0, 256), LB, A("rmask", 0, 1))
-        for m in (0, 2, 1):
-            h1, h2, HBm = A("h1_%d" % m), A("h2_%d" % m), A("HB", 256 * m, 256 * m + 256)
-            P = "P%d" % m
-            mm(A(P, 0, 256), A("SEL%d" % m), A("Bz"), True, True)
-            tt(h1, A(P, 0, 256), LVv, O.add)
-            ts(h2, h1, 255, O.bitwise_and)
-            cp(HBm, h2)
-            s = (t + 1 + m) & 3
-            mms([(A(P, 256, 512), A("cr", 128 * s, 128 * s + 128, 1, slice(0, 1)), ONE1, True, False),
-                 (A(P, 256, 512), A("BMq"), HBm, False, True)])
-        tt(S, A("P5", 0, 256), pool, O.max)
-        quarter(A("DI"), S)
-        PD = A("P5", 256, 512)
-        mms([(A("P6", 0, 48), W(y), A("HB", y, 768, 16), y == 0, y == 15) for y in range(16)])
-        ts(A("Lf"), A("P6", 0, 48), 0.0625, O.mult)
-        cp(PD, A("DI"))
-        OS, OL = "OS%d" % t, "OL%d" % t
-        for m in (0, 2, 1):
-            J = A("P%d" % m, 256, 512)
-            tag[0] = "look%d" % m
-            look(A(OS, 0, 256) if m == 2 else A("OFF%d" % m), PD, S, J, m)
-            if m == 2:
-                cp(A(OS, 256, 272), A("Lf", 32, 48))
-                send(q, A(OL), A(OS), "ro%d" % t)
-        tag[0] = "g0"
-        k0 = [pull("OFF0", 128 * h, 128) for h in range(2)]
-        ts(A("p01", 0, 16), A("Lf", 0, 16), float(c0), O.add)
-        ts(A("p01", 16, 32), A("Lf", 16, 32), float(c1), O.add)
-        cp(A("LV"), A("Lf", 0, 32))
-        tag[0] = "dd0"
-        dedup(0)
-        tag[0] = "j0"
-        for h in range(2):
-            judge("P3", 128 * h, "SMb", 4096 * h, 128, k0[h])
-        if t == 0:
-            first_worth(3)
-        bw, vw, ha, he, hcb, hdb = hostw[t]
-        recv(A(OL), "ro%d" % t, p)
-        tag[0] = "cs"
-        clsB, clsV = A(bw, ha + hcb, ha + hcb + 256), A(vw, ha + hcb, ha + hcb + 256)
-        act(A("CS%d" % t), IND(clsB, A(OL, 256, 272)))
-        send(p, A("BW", Sblk[t] + 256, Sblk[t] + 512), A("CS%d" % t), "rc%d" % t)
-        tag[0] = "g2"
-        k2 = [pull(OL, 128 * h, 128, "S", 2) for h in range(2)]
-        tag[0] = "vj2"
-        act(A("VJ2"), IND(clsV, A(OL, 256, 272)))
-        tag[0] = "c0"
-        tt(A("D01", 0, 256), A("P0", 0, 256), A("THR"), O.is_ge)
-        ts(A("D8", 0, 256), A("D01", 0, 256), 8192.0, O.mult)
-        tt(A("VJ0"), IND(A("VW", wa + c0, wa + c0 + 256), A("LV", 0, 16)), A("D8", 0, 256), O.add)
-        tt(A("CM0", 0, 256), A("P3", 0, 256), A("VJ0"), O.is_gt)
-        act(A("P0", 0, 256), A("CM0", 0, 256))
+        wa = 768 * t
+        tag[1] = t
+        LB, LV = first[t]
+        S = ("BW", wa + slot[3])
+        far = (A("BW", wa + slot[2], wa + slot[2] + 256), A("VM", wa + slot[2], wa + slot[2] + 256))
+        tag[0] = "pool"
         if t > 0:
-            host_change(t - 1)
-        tag[0] = "j2"
+            recv(A("PL%d" % (t - 1), 0, 128), "rp%d" % (t - 1), back(1))
+            recv(A("PL%d" % (t - 1), 128, 256), "rq%d" % (t - 1), back(1))
         for h in range(2):
-            judge("P5", 128 * h, "SM2", 2048 * h, 128, k2[h])
-        tt(A("KS%d" % t), A("P5", 0, 256), A("VJ2"), O.is_gt)
-        send(p, A("KL%d" % t), A("KS%d" % t), "rk%d" % t)
-        tag[0] = "dd1"
-        dedup(1)
-        tag[0] = "dd2"
-        dedup(2)
-        tt(A("D01", 256, 512), A("P1", 0, 256), A("THR"), O.is_ge)
-        ts(A("D8", 256, 512), A("D01", 256, 512), 8192.0, O.mult)
+            lo, hi = 128 * h, 128 * h + 128
+            tag[0] = "pool"
+            ps = A("P7", 256 + lo, 256 + hi)
+            if t > 0:
+                mms([(ps, A("R15"), A("PL%d" % (t - 1), lo, hi))])
+            scale(A("LM", lo, hi), sub(LB, lo, hi), A("col", 4, 5), A("col", 7 if t else 3, 8 if t else 4))
+            tt(sub(S, lo, hi), ps, A("LM", lo, hi), O.add if t else O.max)
+            lin(A("DS", lo, hi), sub(S, lo, hi), 0.25, -74.5)
+            tag[0] = "hash%d" % h
+            ts(A("Bz", lo, hi), sub(LB, lo, hi), 39.0, O.max, 216.0 + 13 * t, O.add)
+            pv = A("P3", 256 + lo, 256 + hi)
+            mms([(pv, A("BM"), sub(LV, lo, hi))])
+            tt(A("h2", lo, hi), pv, A("Bz", lo, hi), O.add)
+            ts(A("h2", lo, hi), A("h2", lo, hi), 255, O.bitwise_and)
+            ts(A("HH", lo, hi), A("h2", lo, hi), A("cls", t, t + 1), O.add)
+            for m in range(3):
+                s = (t + 1 + m) & 3
+                J = A(("P2", "P3", "P7")[m], lo, hi)
+                tag[0] = "look%d%d" % (m, h)
+                mms([(J, A("SEL", 128 * m, 128 * m + 128), A("HH", lo, hi))])
+                tag[0] = "list"
+                lin(A("HB", 256 * m + lo, 256 * m + hi), J, 0.25, -0.25 * (s + 1))
+                tag[0] = "look%d%d" % (m, h)
+                look(A("OFF", 256 * m + lo, 256 * m + hi), A("DS", lo, hi), sub(S, lo, hi), J)
+        tag[0] = "list"
+        mms([(A("P6", 0, 48), W(y), A("HB", y, 768, 16)) for y in range(16)])
+        ts(A("Lf"), A("P6", 0, 48), 0.0625, O.mult)
+        cp(A("LV"), A("Lf"))
+        tt(A("PAY"), A("Lf"), A("PAYc"), O.add)
         if t == 0:
+            first_worth(1)
+            first_worth(3)
+            tag[0] = "rb"
+            send(back(1), far[0], A("C3"), "rb0")
+            send(back(1), far[1], A("V3"), "rv0")
             first_worth(2)
-        tag[0] = "vj1"
-        tt(A("VJ1"), IND(A("VW", wa + c1, wa + c1 + 256), A("LV", 16, 32)), A("D8", 256, 512), O.add)
-        tt(A("P2", 256, 512), A("P2", 0, 256), A("THR"), O.is_lt)
-        recv(A("KL%d" % t), "rk%d" % t, q)
-        tag[0] = "pre"
-        tt(A("CM0", 256, 512), A("KL%d" % t), A("P2", 256, 512), O.mult)
-        mms([(A("P6", 64, 96), W(y), A("CM0", y, 512, 16), y == 0, y == 15) for y in range(16)])
-        tt(A("P0", 0, 256), A("P0", 0, 256), A("CM0", 256, 512), O.max)
-        act(A("E02"), A("P6", 64, 96))
-        e0, e2 = A("E02", 0, 16), A("E02", 16, 32)
-        ts(DC(0), e0, 1.0, O.add)
-        tt(DC(0), DC(0), e2, O.max)
-        ts(DC(2), e0, 0.0, O.is_gt)
-        ts(DC(1), A("I1"), float(so), O.add)
-        tt(DC(3), A("p01", 0, 16), DC(1), O.subtract)
-        tt(DC(3), DC(3), DC(2), O.mult)
-        tt(DC(3), DC(3), DC(1), O.add)
-        tt(DC(4), e2, e0, O.is_gt)
-        ts(DC(1), DC(1), 256.0, O.add)
-        tt(DC(5), DC(1), DC(3), O.subtract)
-        tt(DC(5), DC(5), DC(4), O.mult)
-        tt(DC(5), DC(5), DC(3), O.add)
-        tt(DC(6), A("p01", 16, 32), DC(5), O.subtract)
-        ts(DC(7), e0, -1.0, O.add, 0.0, O.max)
-        tt(DC(7), DC(7), A("I8"), O.add)
-        tt(DC(8), A("I8"), DC(7), O.subtract)
-        ts(DC(8), DC(8), 2047.0, O.add)
-        ts(DC(9), A("I1"), float(hdb), O.add)
-        tt(DC(10), A("Lf", 32, 48), DC(9), O.subtract)
-        ts(DC(10), DC(10), float(hcb), O.add)
-        tt(DC(10), DC(10), DC(4), O.mult)
-        tt(DC(9), DC(9), DC(10), O.add)
-        ts(DC(11), e2, -1.0, O.add, 0.0, O.max)
-        XS = "XS%d" % t
-        tt(A(XS, 272, 288), DC(11), A("I16"), O.add)
-        win = A("BW", wa, we)
-        recv(A("BW", Sblk[t] + 256, Sblk[t] + 512), "rc%d" % t, q)
-        for h in range(2):
-            lo, hi, bank, fb = 128 * h, 128 * h + 128, ("P4", "P5")[h], ("P3", "P4")[h]
-            at = lo
-            tag[0] = "j1%d" % h
-            for n in ([128], [64, 64])[h]:
-                judge(bank, at - lo, "SMb", 2048 + 2048 * h + 16 * at, n, pull("OFF1", at, n, "S", 1))
-                at += n
-            H = lambda k: A("dec", 16 * k + 8 * h, 16 * k + 8 * h + 8)
-            tag[0] = "dec%d" % h
-            tt(A("CM1", lo, hi), A(bank, 0, 128), A("VJ1", lo, hi), O.is_gt)
-            wrap(96, "CM1", 0, 8 * h, 8 * h + 8)
-            tt(A("CMB", lo, hi), A("P0", lo, hi), A("CM1", lo, hi), O.max)
-            mms([(A(fb, 256, 384), A("r15", 0, 128, 1, slice(0, 1)), ONEh, True, False),
-                 (A(fb, 256, 384), A("BID"), A("CMB", lo, hi), False, True),
-                 (A(fb, 384, 512), A("ONE", 0, 128, 1, slice(0, 1)), ONEh, True, False),
-                 (A(fb, 384, 512), A("NSH"), A("CMB", lo, hi), False, True)])
-            E1 = A("P6", 96 + 8 * h, 104 + 8 * h)
-            j = 16 * (13 + h)
-            d13, d14 = A("dec", j, j + 8), A("dec", j + 8, j + 16)
-            tt(H(12), E1, H(0), O.is_ge)
-            tt(d14, E1, H(8), O.add)
-            tt(d13, H(12), H(6), O.mult)
-            tt(d14, d14, H(12), O.mult)
-            tt(d13, d13, H(5), O.add)
-            tt(d14, d14, H(7), O.add)
-            cp(A("IDX", 16 * h, 16 * h + 16), A("dec", j, j + 16))
-            iu, iv = A("IDX", 16 * h, 16 * h + 8), A("IDX", 16 * h + 8, 16 * h + 16)
-            U = sub(newl[t][0], lo, hi)
-            act(U, IND(win, iu))
-            act(A("SMg", lo, hi), IND(A("SMb", 4096 * h, 4096 * h + 4096), iv))
-            mm(A("P7", 256 + lo, 256 + hi), A("BM"), A("SMg", lo, hi), True, True)
-            tt(A("Ys", lo, hi), A(fb, 256, 384), sub(lead[t][0], lo, hi), O.mult)
-            mm(A("P6", 256 + lo, 256 + hi), A("R15"), A("Ys", lo, hi), True, True)
-            act(A("PS%d" % t, lo, hi), A("P6", 256 + lo, 256 + hi))
-            tt(A(XS, lo, hi), A(fb, 384, 512), A("BW", Sblk[t] + lo, Sblk[t] + hi), O.mult)
-            act(A("VN", lo, hi), A("P7", 256 + lo, 256 + hi))
-            tag[0] = "sc%d" % h
-            cp(IND(win, iu), A(XS, lo, hi))
-            cp(IND(A("VW", wa, we), iu), A("VN", lo, hi))
-            if h == 1:
-                send(nxt, A("PL%d" % t), A("PS%d" % t), "rp%d" % t)
-                tt(DC(12), DC(12), DC(10), O.mult)
-                tt(A(XS, 256, 272), DC(9), DC(12), O.subtract)
-                send(q, A("XL%d" % t), A(XS), "rx%d" % t)
-            tag[0] = "ol%d" % h
-            quarter(A("DIo", lo, hi), U)
-            look(A("OFFO", lo, hi), A("DIo", lo, hi), U, A("JC", 256 * t + lo, 256 * t + hi), 3)
-            for a in (lo, lo + 64) if t + 1 == RO else (lo,):
-                n = 64 if t + 1 == RO else 128
-                worth("OFFO", a, sub(newl[t][1], a, a + n), a, n, "V" if t + 1 == RO and a % 128 else "S")
+        tag[0] = "vj2"
+        recv(A("TB%d" % (t + 1)), "rt%d" % t, helper(ahead(t + 1)) if t else ahead(1), CP["tab"] * (t + 1))
+        recv(far[0], "rb%d" % t, ahead(t + 1))
+        recv(far[1], "rv%d" % t, ahead(t + 1))
+        if t > 0:
+            recv(sub(home[t - 1][0], 0, 256), "bb%d" % (t - 1), back(t))
+            recv(sub(home[t - 1][1], 0, 256), "bv%d" % (t - 1), back(t))
+        def eb(m, k):
+            return 6144 * (k >> 3) + 256 * (8 * m + (k & 7))
 
-    recv(A("PL%d" % (RO - 1)), "rp%d" % (RO - 1), prv)
-    host_change(RO - 1)
-    fb = {0: newl[0][0], 1: newl[1][0], 2: newl[2][0], 3: ("BW", 1792)}
-    fv = {0: newl[0][1], 1: newl[1][1], 2: newl[2][1], 3: ("VW", 1792)}
+        for m in range(3):
+            tag[0] = "dd%d" % m
+            for k in range(16):
+                ts(A("EB", eb(m, k), eb(m, k) + 256 - 16 * k), A("HB", 256 * m + 16 * k, 256 * m + 256), A("Lf", 16 * m + k, 16 * m + k + 1), O.is_equal)
+            for h in range(2):
+                l = []
+                for k in range(8 * h + 7):
+                    a = max(128 * h, 16 * k + 16)
+                    l.append((A("P%d" % h, 128 * (m - h) + a, 128 * m + 128), A("BM8"), A("EB", eb(m, k) + a - 16 * k, eb(m, k) + 128 * h + 128 - 16 * k)))
+                if h == 0:
+                    l.insert(0, (A("P0", 128 * m, 128 * m + 16), A("BM8"), A("ZR")))
+                for k in range(0, len(l), 4):
+                    mms(l[k:k + 4], ("P", t, h), False)
+                    if k == 0:
+                        ops[-1]["use"].append((A("P%d" % h, 128 * m, 128 * m + 128), 1))
+            tag[0] = "vj%d" % m
+            move(A("VJ", 256 * m, 256 * m + 256), IND(A("VM", wa + slot[m], wa + slot[m] + 256), A("LV", 16 * m, 16 * m + 16)))
+            for h in range(2):
+                mms([(A("P%d" % h, 128 * m, 128 * m + 128), A("BMn"), A("VJ", 256 * m + 128 * h, 256 * m + 128 * h + 128))], ("P", t, h), False)
+        tag[0] = "dd2"
+        for h in range(2):
+            for x in range(1, 16, 5):
+                mms([(A("P%d" % h, j, 369 + j, 16), A("TRI", 128 * j, 128 * j + 128), A("EB", 6144 * h + j, 6144 * h + j + 23 * 256 + 1, 256))
+                     for j in range(x, x + 5)], ("P", t, h), False)
+        win, vwin = A("BW", wa, wa + 1024), A("VM", wa, wa + 1024)
+        for h in range(2):
+            lo, hi, SM, P = 128 * h, 128 * h + 128, "SM%d" % h, "P%d" % h
+            for m in range(3):
+                tag[0] = "j%d%d" % (m, h)
+                for a in range(0, 128, CH):
+                    b = 2048 * (2 - m) + 16 * a
+                    sights("TB%d" % (t + 1 if m == 2 else 0), "OFF", 256 * m + lo + a, SM, b, 1)
+                    mms([(A(P, 128 * m + a, 128 * m + a + CH), W(d), A(SM, b + d, b + 16 * CH, 16)) for d in range(16)], ("P", t, h), False)
+                    ops[-1]["tag"] += "s"
+            tag[0] = "dec%d" % h
+            C = [A("CM", 256 * m + lo, 256 * m + hi) for m in range(3)]
+            for m in range(3):
+                ts(C[m], A(P, 128 * m, 128 * m + 128), 0.0, O.is_gt, 8192.0, O.mult)
+                ops[-1]["use"].append((A(P, 0, 384), 0))
+            E = A("P6", 64 + 64 * h, 112 + 64 * h)
+            mms([(E, W(y), A("CM", y, 768, 16)) for y in range(16)])
+            Q, Rr = A("P5", 0, 128), A("P5", 128, 256)
+            mms([(Rr, A("BID"), C[m]) for m in range(3)])
+            mms([(Q, A("NSH"), C[m]) for m in range(3)])
+            tt(A("KS", 0, 48), E, A("PAY"), O.add)
+            tt(A("K1"), A("KS", 0, 32), A("KS", 32, 64), O.max)
+            kb = A("KB", 32, 40)
+            tt(kb, A("K1", 8 * h, 8 * h + 8), A("K1", 16 + 8 * h, 24 + 8 * h), O.max)
+            ts(A("KB", 16 * h, 16 * h + 8), kb, 1023, O.bitwise_and)
+            cp(A("IDX", 16 * h, 16 * h + 8), A("KB", 16 * h, 16 * h + 8))
+            ts(A("KB", 16 * h + 8, 16 * h + 16), kb, 13, O.arith_shift_right)
+            ts(A("KB", 40, 48), kb, 6144, O.bitwise_and)
+            tt(A("KB", 40, 48), A("KB", 40, 48), A("KB", 16 * h + 8, 16 * h + 16), O.add)
+            cp(A("IDX", 16 * h + 8, 16 * h + 16), A("KB", 40, 48))
+            iu, iv = A("IDX", 16 * h, 16 * h + 8), A("IDX", 16 * h + 8, 16 * h + 16)
+            U = A("UB%d" % t, lo, hi)
+            tag[0] = "ys%d" % h
+            lin(A("Ys", lo, hi), sub(LB, lo, hi), 1.0, -2344.0)
+            ts(Rr, Rr, A("col", 6, 7), O.is_gt)
+            tt(A("PS%d" % t, lo, hi), Rr, A("Ys", lo, hi), O.mult)
+            tag[0] = "sc%d" % h
+            tt(A("XS", lo, hi), Q, sub(S, lo, hi), O.add)
+            move(U, IND(win, iu))
+            move(A("SMg", lo, hi), IND(A(SM), iv))
+            cp(IND(win, iu), A("XS", lo, hi))
+            cp(IND(vwin, iu), A("SMg", lo, hi))
+            tag[0] = "rp"
+            send(ahead(1), A("PL%d" % t, lo, hi), A("PS%d" % t, lo, hi), "r%s%d" % ("pq"[h], t))
+            if h == 1:
+                tag[0] = "bb"
+                send(ahead(t + 1), sub(home[t][1], 0, 256), far[1], "bv%d" % t)
+                send(ahead(t + 1), sub(home[t][0], 0, 256), far[0], "bb%d" % t, [sent["bv%d" % t]] if t + 1 < RO else [])
+            tag[0] = "own%d" % h
+            mine(U, t, lo, 128, A("P%d" % (5 + h), 256, 384), "OFFO", lo, A("VU%d" % t, lo, hi), 16 * lo)
+        if t + 1 < RO:
+            tag[0] = "rb"
+            a = wa + 768 + slot[2]
+            send(back(t + 2), A("BW", a, a + 256), A("UB%d" % t), "rb%d" % (t + 1), [sent["bb%d" % t]])
+            send(back(t + 2), A("VM", a, a + 256), A("VU%d" % t), "rv%d" % (t + 1))
+
     tag[0] = "out"
-    ts(A("PO"), A("PL%d" % (RO - 1)), -296.0, O.add, -1.0, O.max)
-    dma("Y", (T.yp[:], None, 0, 0), (T.PO[15::16, :], "PO", 0, 256))
+    last = RO - 1
+    recv(A("PL%d" % last, 0, 128), "rp%d" % last, back(1))
+    recv(A("PL%d" % last, 128, 256), "rq%d" % last, back(1))
+    recv(A("C1b"), "bb%d" % last, back(RO))
+    recv(A("V1b"), "bv%d" % last, back(RO))
+    fin = [home[1], home[2], (("UB2", 0), ("VU2", 0)), home[0]]
+    g8 = slice(0, 8)
+    mms([(A("P3", 0, 256, 1, g8), A("G8f"), A("PL%d" % last))])
+    ts(A("PO", 0, 256, 1, g8), A("P3", 0, 256, 1, g8), 2344.0 - 296.0, O.add, -1.0, O.max)
+    dma("S", hbm(T.yp[:]), A("PO", 0, 256, 1, g8))
     for s in range(4):
-        ts(A("OUT", s, 1021 + s, 4), sub(fb[s], 0, 256), -296.0, O.add, -1.0, O.max)
-        act(A("OUTV", s, 1021 + s, 4), sub(fv[s], 0, 256))
-    dma("Y", (T.yb[:], None, 0, 0), A("OUT"))
-    dma("Y", (T.yv[:], None, 0, 0), (T.OUTV[0::16, :], "OUTV", 0, 1024))
+        ts(A("OUT", s, 1021 + s, 4), sub(fin[s][0], 0, 256), -296.0, O.add, -1.0, O.max)
+        pv = A("P%d" % (s & 1), 256 * (s >> 1), 256 * (s >> 1) + 256, 1, g8)
+        mms([(pv, A("G8"), sub(fin[s][1], 0, 256))])
+        move(A("OUTV", s, 1021 + s, 4, g8), pv)
+    dma("Y", hbm(T.yb[:]), A("OUT"))
+    dma("Y", hbm(T.yv[:]), A("OUTV", 0, 1024, 1, g8))
 
     if not _order:
         _order["o"] = arrange(ops, needs(ops))
-    for i in _order["o"]:
-        issue(ops[i])
+    for i, q in _order["o"]:
+        issue(ops[i], q)
     for s in sorted(cnt):
         if cnt[s]:
             g.wait_ge(T.sem[s], cnt[s])

from concourse.mybir import AluOpType as O, ActivationFunctionType as F

RO = 3
f32, b16, f16, i32, u16 = "float32", "bfloat16", "float16", "int32", "uint16"
SCRATCH = {}
CH = 64
NG = 10
HW = 6144


def _b(name, cols, dtype, where="sbuf"):
    SCRATCH[name] = (where, [128, cols], dtype)


for _k in range(8):
    _b("P%d" % _k, 512, f32, "psum")
for _n, _c, _d in [
    ("bunI", 1024, i32), ("potI", 256, i32), ("R01", 16 * CH, b16), ("IX", 256, b16),
    ("ip", 128, i32), ("ic", 128, i32), ("id0", 128, i32), ("q1", 128, i32), ("q2", 128, i32), ("q3", 128, i32),
    ("BM", 128, b16), ("BMn", 128, b16), ("BM8", 128, b16), ("WX", 2048, b16), ("TRI", 2048, b16), ("ONE", 16, b16), ("ZR", 16, b16),
    ("KJ", 512, b16), ("cls", 3, f32), ("G8", 8, b16), ("G8f", 8, f16), ("LT", 16, f32),
    ("SEL", 384, f16), ("R15", 128, f16), ("LM", 256, f32), ("NSH", 128, b16), ("BID", 128, b16),
    ("k1", 128, b16), ("k2", 128, b16), ("col", 8, f32), ("wk", 40, i32), ("I1", 32, f32), ("PAYc", 48, f32),
    ("L0", 256, f32), ("C3", 256, f32), ("V0", 256, b16), ("V3", 256, b16), ("BW", 2560, f32), ("VM", 2560, b16),
    ("C1b", 256, f32), ("V1b", 256, b16), ("Bz", 256, f32), ("DS", 256, f32), ("DO", 512, f32),
    ("HH", 256, f16), ("HB", 768, b16), ("Lf", 48, f32), ("LV", 48, u16), ("PAY", 48, f32), ("EB", 3 * 4096, b16), ("VJ", 768, b16),
    ("SM0", HW, b16), ("SM1", HW, b16), ("SMo", 8192, b16), ("CM", 768, b16), ("KS", 64, f32), ("K1", 32, f32), ("KB", 48, i32),
    ("IDX", 32, u16), ("Ys", 256, f32), ("XS", 256, f32), ("SMg", 256, b16),
    ("OFFO", 256, u16), ("OFFI", 1024, u16), ("OFF", 768, u16), ("OUT", 1024, f32), ("OUTV", 1024, f32), ("PO", 256, f32),
    ("GR", NG * 16 * CH, b16), ("h1", 1024, i32), ("h2", 256, i32),
]:
    _b(_n, _c, _d)
for _k in range(RO + 1):
    _b("TB%d" % _k, 2064, b16)
for _k in range(RO):
    _b("UB%d" % _k, 256, f32)
    _b("VU%d" % _k, 256, b16)
    _b("PS%d" % _k, 256, f16)
    _b("PL%d" % _k, 256, f16)
SEMAPHORES = ["v", "s", "t", "gp", "ls", "rh"] + ["d%d" % k for k in range(12)] + ["%s%d" % (n, k) for n in ("rt", "rb", "rv", "bb", "bv", "rp", "rq") for k in range(RO)]
CP = {"cy": 0.9e-3, "pe": 0.6e-3, "gat": 1.5, "sca": 3.5, "rem": 4.5, "tab": 14.0, "lat": 0.15, "look": 0.05, "bias": 0.5}
BOOST = {"io": -50, "const": 60, "rt": 5, "init0": -20, "init0g": -20, "init0s": -20, "init1": -10, "init1g": 2, "init1s": 6, "init3": -8, "init3g": 1,
         "init3s": 4, "init2": 5, "init2g": 11.5, "init2s": 12, "pool": 0, "hash0": 0, "hash1": 2, "look00": 1, "look10": 3, "look20": 5, "look01": 7,
         "look11": 8, "look21": 9, "list": 3.5, "dd0": 6, "dd1": 6.2, "dd2": 6.4, "vj0": 9, "vj1": 9.2, "vj2": 12.2, "j00g": 10, "j10g": 11, "j20g": 12,
         "j01g": 20, "j11g": 21, "j21g": 22, "j00s": 5.5, "j10s": 10, "j20s": 12.1, "j01s": 20.5, "j11s": 21.5, "j21s": 22.5, "dec0": 13, "ys0": 14,
         "sc0": 14.5, "own0": 15, "own0g": 90, "own0s": 104, "dec1": 30, "ys1": 30.5, "sc1": 32, "own1": 33, "own1g": 95, "own1s": 104.5,
         "rp": 31, "bb": 40, "rb": 105, "out": 150}
BOOST.update({'init1s': -1.1, 'init3g': -5.4, 'init3s': 18.4, 'pool': -4.0, 'hash1': 1.0, 'look00': 2.2, 'look20': 4.7, 'look01': 9.1, 'look11': 3.6, 'dd2': 0.8, 'j10g': 8.2, 'j20g': 12.3, 'j00s': 4.8, 'j10s': 7.3, 'j11s': 18.7, 'j21s': 30.8, 'ys0': 13.4, 'own0g': 86.2, 'own0s': 101.8, 'dec1': 35.2, 'own1': 28.8, 'own1s': 106.9, 'bb': 32.6})
BYV = [12, 15, 20, 29, 40, 49, 57, 62]
_order = {}


def clash(w, w2):
    return (w or w2) and not (w == 2 and w2 == 2)


def needs(ops):
    dep = [set() for _ in ops]
    hist = {}
    for i, o in enumerate(ops):
        dep[i].update(o["after"])
        for x, w in o["use"]:
            for (l, h, w2, k) in hist.get(x[1], ()):
                if k != i and clash(w, w2) and l < x[3] and h > x[2]:
                    dep[i].add(k)
        for x, w in o["use"]:
            if w == 1:
                hist[x[1]] = [r for r in hist.get(x[1], []) if not (r[0] >= x[2] and r[1] <= x[3])]
            hist.setdefault(x[1], []).append((x[2], x[3], w, i))
    return dep


def lay(ops, dep, suc, pr, fwd):
    n = len(ops)
    left = [len(d) for d in dep]
    rdy = [0.0] * n
    at = [0.0] * n
    free = {}
    bank = {}
    pool = [i for i in range(n) if not left[i]]
    order = []

    def when(i, q):
        return max([rdy[i]] + [bank[b][0] for b in ops[i]["banks"] if b in bank and bank[b][1] != q])

    while pool:
        best = None
        for q in "RYGTSV":
            c = [(when(i, q), i) for i in pool if q in ops[i]["var"]]
            if not c:
                continue
            t = max(free.get(q, 0.0), min(c)[0])
            if best is None or t < best[0]:
                w, k = max((x for x in c if x[0] <= t + CP["look"]),
                           key=lambda x: pr[x[1]] - (CP["bias"] if q == "V" and len(ops[x[1]]["var"]) > 1 else 0.0))
                best = (t, q, k, max(t, w))
        _, q, i, t = best
        pool.remove(i)
        order.append((i, q))
        end = t + ops[i]["var"][q][1]
        at[i] = end
        free[q] = end if q != "R" else 0.0
        for b in ops[i]["banks"]:
            bank[b] = (end + CP["lat"], q)
        for k in suc[i]:
            rdy[k] = max(rdy[k], end + ops[i if fwd else k]["lat"])
            left[k] -= 1
            if not left[k]:
                pool.append(k)
    return order, at, max(at[i] + ops[i]["lat"] for i in range(n))


def arrange(ops, dep):
    n = len(ops)
    suc = [[] for _ in range(n)]
    for i in range(n):
        for k in dep[i]:
            suc[k].append(i)
    pr = [0.0] * n
    for i in range(n - 1, -1, -1):
        pr[i] = max([-100.0 * ops[i]["round"] - BOOST[ops[i]["tag"]]] + [pr[k] for k in suc[i]]) + 1e-3
    return lay(ops, dep, suc, pr, True)[0]


def rank_program(g, core, T, topo):
    N = len(T.cores)

    def helper(c):
        return [x for x in topo.cores_of(c) if topo.die(x) != topo.die(c)][0]

    def inner(c):
        far = [topo.engines(c, x) for x in T.cores if x != c]
        return [e for e in topo.engines(c, helper(c)) if not any(e in f for f in far)]

    rank = T.rank_of(core)
    if rank is None:
        for r, c in enumerate(T.cores):
            if helper(c) == core:
                g.wait_ge(T.sem.rh, len(inner(c)))
                out = 0
                for t in range(1, RO):
                    dst = T.cores[(r - 1 - t) % N]
                    rid, pid = topo.addr(dst, core)
                    g.remote_dma(T["TB%d" % (t + 1)][:], T.TB0[:], T.sem["rt%d" % t], T.sem.ls, pid, rid, topo.mask(core, dst))
                    out += len(topo.engines(core, dst))
                g.wait_ge(T.sem.ls, out)
        return
    eng = {"V": g.vector, "S": g.scalar, "T": g.tensor, "Y": g.sync, "G": g}
    own = {"V": "v", "S": "s", "T": "t", "G": "gp"}
    cnt = {"v": 0, "s": 0, "t": 0, "gp": 0, "ls": 0}
    know = {q: {} for q in eng}
    recs = {}
    nd = [0]
    ring = [0, 0]
    tag = ["", 0]
    ops = []
    sent = {}
    todo = {}
    begun = set()
    cy = CP["cy"]

    def A(n, lo=0, hi=None, st=1, ps=slice(None)):
        if hi is None:
            hi = T[n].shape[1]
        return (T[n][ps, lo:hi:st], n, lo, hi)

    def sub(x, lo, hi):
        return A(x[0], x[1] + lo, x[1] + hi)

    def hbm(ap):
        return (ap, None, 0, 0)

    def cols(x):
        return x[0].shape[1]

    def IND(w, o):
        return (w[0].indirect(o[0]), [w, o])

    def ind(x):
        return isinstance(x[1], list)

    def psum(x):
        return x[1] in SCRATCH and SCRATCH[x[1]][0] == "psum"

    def two(x):
        return SCRATCH[x[1]][2] in (b16, f16, u16)

    def add(var, outs, ins, lat=None, after=(), kind="c", more=()):
        use = list(more)
        for lst, w in ((ins, 0), (outs, 1)):
            for x in lst:
                if ind(x):
                    use += [(x[1][0], w), (x[1][1], 0)]
                elif x[1] is not None:
                    use.append((x, w))
        ops.append({"var": var, "use": use, "lat": CP["lat"] if lat is None else lat, "after": list(after), "kind": kind, "tag": tag[0], "round": tag[1],
                    "banks": sorted(set(x[1] for x, w in use if psum(x)))})

    def plain(o, a):
        return max(64, cols(a) * (0.5 if two(o) and two(a) else 1)) * cy

    def tt(o, a, b, op):
        c = max(64, cols(a) * (1 if psum(a) or psum(b) else 2)) * cy
        add({"V": ([lambda: g.vector.tensor_tensor(o[0], a[0], b[0], op)], c)}, [o], [a, b])

    def vts(o, a, s1, op0, s2=None, op1=None):
        v1 = s1[0] if isinstance(s1, tuple) else s1
        if op1 is None:
            return [lambda: g.vector.tensor_scalar(o[0], a[0], v1, None, op0)], plain(o, a)
        return [lambda: g.vector.tensor_scalar(o[0], a[0], v1, s2, op0, op1)], plain(o, a)

    def ts(o, a, s1, op0, s2=None, op1=None):
        add({"V": vts(o, a, s1, op0, s2, op1)}, [o], [a] + ([s1] if isinstance(s1, tuple) else []))

    def cp(o, a):
        c = 0.06 + 16 * cols(o[1][1]) * CP["sca"] * cy if ind(o) else plain(o, a)
        add({"V": ([lambda: g.vector.tensor_copy(o[0], a[0])], c)}, [o], [a])

    def fill(o, c):
        add({"V": ([lambda: g.vector.memset(o[0], c)], plain(o, o))}, [o], [])

    def move(o, a):
        c = 0.06 + 16 * cols(a[1][1]) * CP["gat"] * cy if ind(a) else None
        add({"V": ([lambda: g.vector.tensor_copy(o[0], a[0])], c or plain(o, a)),
             "S": ([lambda: g.scalar.activation(o[0], a[0], F.Copy)], c or max(64, cols(a)) * cy)}, [o], [a])

    def lin(o, a, m, c):
        add({"V": vts(o, a, m, O.mult, c, O.add),
             "S": ([lambda: g.scalar.activation(o[0], a[0], F.Identity, c, m)], max(64, cols(a)) * cy)}, [o], [a])

    def scale(o, a, m, c):
        add({"V": vts(o, a, m, O.mult, c[0], O.add),
             "S": ([lambda: g.scalar.activation(o[0], a[0], F.Identity, c[0], m[0])], max(64, cols(a)) * cy)}, [o], [a, m, c])

    def relu(o, a, c):
        add({"V": vts(o, a, c, O.add, 0.0, O.max),
             "S": ([lambda: g.scalar.activation(o[0], a[0], F.Relu, c, 1.0)], max(64, cols(a)) * cy)}, [o], [a])

    def mms(lst, grp=None, first=True):
        bank = lst[0][0][1]
        key = grp or ("g", len(ops))
        todo[key] = todo.get(key, 0) + len(lst)

        def one(x):
            def f():
                todo[key] -= 1
                st = key not in begun
                begun.add(key)
                return g.tensor.matmul(x[0][0], x[1][0], x[2][0], st, todo[key] == 0)
            return f
        c = sum(max(min(64, cols(x[1])), cols(x[2])) * (1 if two(x[1]) else 4) for x in lst) * CP["pe"]
        tok = (None, "grp" + bank, 0, 1)
        more = [(tok, 1 if first else 0)] + ([] if first else [(x[0], 2) for x in lst])
        add({"T": ([one(x) for x in lst], c)}, [x[0] for x in lst] if first else [],
            [y for x in lst for y in x[1:3]], more=more)

    def iota(o, pat, base, cm):
        c = 0.15 + 2 * cols(o) * cy
        if SCRATCH[o[1]][2] != i32:
            add({"G": ([lambda: g.iota(o[0], pat, base, cm, allow_small_or_imprecise_dtypes=True)], c)}, [o], [])
        else:
            add({"G": ([lambda: g.iota(o[0], pat, base, cm)], c)}, [o], [])

    def dma(q, out, in_, lat=3.0):
        add({q: ([lambda: eng[q].dma_start(out[0], in_[0])], 0.1)}, [out], [in_], lat, kind="d")

    def send(dst, out, in_, sem, after=()):
        es = inner(core) if dst == helper(core) else topo.engines(core, dst)
        m = sum(1 << e for e in es)
        rid, pid = topo.addr(dst, core)
        cnt["ls"] += len(es)
        sent[sem] = len(ops)
        add({"G": ([lambda: g.remote_dma(out[0], in_[0], T.sem[sem], T.sem.ls, pid, rid, m)], 0.4)}, [], [in_], 0.0, after, "r")

    def recv(out, sem, src, lat=None):
        add({"R": ([(sem, len(topo.engines(src, core)), out)], 0.0)}, [out], [], lat or CP["rem"], [sent[sem]], "v")

    def wait_for(q, use):
        need = []
        for x, w in use:
            n, lo, hi = x[1], x[2], x[3]
            if n not in SCRATCH:
                continue
            ps = psum(x)
            for r in recs.get(n, ()):
                if r[3] == q and q == "T" and ps:
                    continue
                if (ps and r[3] != q) or (r[0] < hi and r[1] > lo and (w or r[2])):
                    need.append(r)
        kn = know[q]
        need = [r for r in need if kn.get(r[4], 0) < r[5]]
        need.sort(key=lambda r: -sum(r[6].values()))
        for r in need:
            if kn.get(r[4], 0) < r[5]:
                eng[q].wait_ge(T.sem[r[4]], r[5])
                for s, v in r[6].items():
                    if kn.get(s, 0) < v:
                        kn[s] = v

    def note(n, lo, hi, w, q, sem, val, clk):
        if n not in SCRATCH:
            return
        if w == 1:
            recs[n] = [r for r in recs.get(n, []) if not (r[0] >= lo and r[1] <= hi)]
        recs.setdefault(n, []).append((lo, hi, w, q, sem, val, clk))

    def issue(o, q):
        fns = o["var"][q][0]
        if o["kind"] == "v":
            sem, ne, x = fns[0]
            cnt[sem] = ne
            note(x[1], x[2], x[3], 1, "R", sem, ne, {sem: ne})
            return
        wait_for(q, o["use"])
        if o["kind"] == "r":
            fns[0]()
            return
        if o["kind"] == "d":
            s, by = "d%d" % nd[0], "D"
            nd[0] += 1
            cnt[s] = 16
            fns[0]().then_inc(T.sem[s], 16)
        else:
            s, by = own[q], q
            for f in fns:
                cnt[s] += 1
                f().then_inc(T.sem[s], 1)
        clk = dict(know[q])
        clk[s] = cnt[s]
        for x, w in o["use"]:
            note(x[1], x[2], x[3], w, by, s, cnt[s], clk)

    def sights(tab, off, lo, dst, first, step):
        k = 16 * CH * (ring[0] % NG)
        ring[0] += 1
        n = 16 * CH
        move(A("GR", k, k + n), IND(A(tab), A(off, lo, lo + CH)))
        del ops[-1]["var"]["S" if ring[0] - 1 in BYV else "V"]
        ops[-1]["tag"] += "g"
        e = first + step * (n - 1)
        o = (T[dst][:, e:(first - step if first >= step else None):-step], dst, first, e + 1)
        d = (T.GR[:, k + n - 1:(k - 1 if k else None):-1], "GR", k, k + n)
        z = A("R01")
        add({"V": ([lambda: g.vector.tensor_tensor_scan(o[0], z[0], d[0], 0.0, O.min, O.max)], n / 2 * cy)}, [o], [z, d])
        ops[-1]["tag"] += "s"

    def W(y):
        return A("WX", 128 * y, 128 * y + 128)

    def back(k):
        return T.cores[(rank - k) % N]

    def ahead(k):
        return T.cores[(rank + k) % N]

    tag[0] = "io"
    dma("Y", A("bunI", 0, 512), hbm(T.bun[:, 0:512]), 4.5)
    dma("S", A("TB0", 37, 2048), hbm(T.sight[:, 0:2011]), 4.0)
    dma("S", A("TB0", 0, 37), hbm(T.sight[:, 2011:2048]), 4.0)
    dma("Y", A("bunI", 512, 1024), hbm(T.bun[:, 512:1024]), 6.0)
    fill(A("potI"), -1)
    dma("Y", (T.potI[15::16, :], "potI", 0, 256), hbm(T.pots[:]), 6.0)
    iota(A("ip"), [[0, 128]], 0, 1)
    iota(A("ic"), [[1, 128]], 0, 0)
    iota(A("id0"), [[-1, 128]], 0, 1)
    iota(A("wk", 0, 16), [[0, 2], [16, 8]], 0, 0)
    iota(A("wk", 16, 32), [[16, 16]], 0, 0)
    iota(A("wk", 32, 35), [[1, 3]], 1, 1)
    iota(A("IX", 0, 256, 1, slice(0, 2)), [[1, 256]], 0, 1)
    for s in range(4):
        iota(A("KJ", 128 * s, 128 * s + 128, 1, slice(0, 2)), [[0, 128]], 3 - s, 2 * s - 2)
    iota(A("R01"), [[0, CH], [256, 16]], 0, 0)
    tag[0] = "const"
    fill(A("TB0", 2048, 2064), 0.0)
    fill(A("ONE"), 1.0)
    fill(A("ZR"), 0.0)
    ts(A("wk", 32, 35), A("wk", 32, 35), 3, O.bitwise_and)
    ts(A("cls"), A("wk", 32, 35), 1.0, O.add, 0.25, O.mult)
    fill(A("WX"), 0.0)
    fill(A("CM"), 0.0)
    for t in range(RO):
        fill(A("VM", 768 * t + 512, 768 * t + 768), 0.0)
    ts(A("q1"), A("ip"), 4, O.arith_shift_right)
    ts(A("q2"), A("ic"), 4, O.arith_shift_right)
    tt(A("BM"), A("q1"), A("q2"), O.is_equal)
    ts(A("q3"), A("ip"), 15, O.bitwise_and)
    for gg in range(8):
        ts(A("WX", 16 * gg, 16 * gg + 15 * 129 + 1, 129), A("ONE", 0, 16), A("BM", 16 * gg, 16 * gg + 1), O.mult)
    ts(A("BMn"), A("BM"), -1.0, O.mult)
    ts(A("BM8"), A("BM"), -8192.0, O.mult)
    cp(A("G8"), A("BM", 0, 128, 16))
    cp(A("G8f"), A("BM", 0, 128, 16))
    for m in range(3):
        ts(A("col", m, m + 1), A("q3", 0, 1), m, O.is_equal, 4.0, O.mult)
        ts(A("SEL", 128 * m, 128 * m + 128), A("BM"), A("col", m, m + 1), O.mult)
    tt(A("LT"), A("q3", 0, 16), A("ic", 0, 16), O.is_lt)
    for x in range(1, 16):
        ts(A("TRI", 128 * x, 128 * x + 128), A("BM8"), A("LT", x, x + 1), O.mult)
    cp(A("R15"), W(15))
    fill(A("col", 3, 4), 0.0)
    ts(A("col", 4, 5), A("q3", 0, 1), 15, O.not_equal)
    ts(A("col", 6, 7), A("col", 4, 5), -1.0, O.add)
    ts(A("col", 7, 8), A("col", 6, 7), -2344.0, O.mult)
    ts(A("k1"), A("id0"), 1, O.is_equal)
    tt(A("k1"), A("k1"), A("BM"), O.mult)
    ts(A("NSH"), A("k1"), -0.625, O.mult)
    ts(A("k2"), A("id0"), 2, O.is_equal, 4.0, O.mult)
    tt(A("k2"), A("k2"), A("BM"), O.mult)
    tt(A("k1"), A("k1"), A("k2"), O.subtract)
    ts(A("col", 5, 6), A("q3", 0, 1), 1, O.is_equal)
    ts(A("k2"), W(15), A("col", 5, 6), O.mult)
    tt(A("k1"), A("k1"), A("k2"), O.subtract)
    ts(A("BID"), A("k1"), 2.0, O.mult)
    tt(A("I1"), A("q3", 0, 32), A("wk", 0, 32), O.add)
    slot = [0, 768, 256, 512]
    for m in range(3):
        ts(A("PAYc", 16 * m, 16 * m + 16), A("I1", 0, 16), 131072.0, O.mult, 2048.0 * (2 - m) - 8192 + slot[m], O.add)
    ts(A("KS", 48, 64), A("I1", 0, 16), 131072.0, O.mult, 4096.0 - 8192 + slot[3], O.add)
    tt(A("KS", 48, 64), A("KS", 48, 64), A("I1", 16, 32), O.add)

    def goods(o, src, pt):
        ts(pt, src, 0, O.is_ge, 296.0, O.mult)
        tt(o, pt, src, O.add)

    def look(o, D, c, J):
        n = cols(c)
        k = 256 * (ring[1] % 4)
        ring[1] += 1
        h1 = A("h1", k, k + n)
        tt(J, c, J, O.mult)
        tt(h1, J, D, O.add)
        ts(h1, h1, 3, O.arith_shift_right, 2047 | (1 << 23), O.bitwise_and)
        ts(o, h1, 2048, O.min)

    def mine(c, s, lo, n, J, off, at, dst, sm):
        D = A("DO", at % 512, at % 512 + n)
        lin(D, c, 0.25, -74.5)
        mms([(J, A("KJ", 128 * s, 128 * s + 128, 1, slice(0, 2)), A("IX", lo, lo + n, 1, slice(0, 2)))])
        look(A(off, at, at + n), D, c, J)
        for a in range(0, n, CH):
            sights("TB0", off, at + a, "SMo", sm + 16 * a, 1)
        move(dst, A("SMo", sm, sm + 16 * n, 16))
        ops[-1]["tag"] += "s"

    tag[0] = "rt"
    send(back(1), A("TB1"), A("TB0"), "rt0")
    send(helper(core), A("TB0"), A("TB0"), "rh", [sent["rt0"]])
    for t in range(1, RO):
        sent["rt%d" % t] = sent["rh"]
    first = {0: (("L0", 0), ("V0", 0)), 1: (("BW", 0), ("VM", 0)), 2: (("BW", 768), ("VM", 768)), 3: (("C3", 0), ("V3", 0))}

    def first_worth(s):
        for h in range(2):
            tag[0] = "init%d" % s
            lo = 128 * h
            bank = "P%d" % (5 + h)
            c = sub(first[s][0], lo, lo + 128)
            goods(c, A("bunI", s + 4 * lo, 4 * lo + 512, 4), A(bank, 384, 512))
            mine(c, s, lo, 128, A(bank, 256, 384), "OFFI", 256 * s + lo, sub(first[s][1], lo, lo + 128), 4096 * (s & 1) + 16 * lo)

    first_worth(0)
    tag[0] = "pool"
    ts(A("P2", 256, 512), A("potI"), 0, O.is_ge, 296.0, O.mult)
    tt(A("P7", 256, 512), A("P2", 256, 512), A("potI"), O.add)
    home = [(("BW", 1536), ("VM", 1536)), (("BW", 2304), ("VM", 2304)), (("C1b", 0), ("V1b", 0))]

    for t in range(RO):
        wa = 768 * t
        tag[1] = t
        LB, LV = first[t]
        S = ("BW", wa + slot[3])
        far = (A("BW", wa + slot[2], wa + slot[2] + 256), A("VM", wa + slot[2], wa + slot[2] + 256))
        tag[0] = "pool"
        if t > 0:
            recv(A("PL%d" % (t - 1), 0, 128), "rp%d" % (t - 1), back(1))
            recv(A("PL%d" % (t - 1), 128, 256), "rq%d" % (t - 1), back(1))
        for h in range(2):
            lo, hi = 128 * h, 128 * h + 128
            tag[0] = "pool"
            ps = A("P7", 256 + lo, 256 + hi)
            if t > 0:
                mms([(ps, A("R15"), A("PL%d" % (t - 1), lo, hi))])
            scale(A("LM", lo, hi), sub(LB, lo, hi), A("col", 4, 5), A("col", 7 if t else 3, 8 if t else 4))
            tt(sub(S, lo, hi), ps, A("LM", lo, hi), O.add if t else O.max)
            lin(A("DS", lo, hi), sub(S, lo, hi), 0.25, -74.5)
            tag[0] = "hash%d" % h
            ts(A("Bz", lo, hi), sub(LB, lo, hi), 39.0, O.max, 216.0 + 13 * t, O.add)
            pv = A("P3", 256 + lo, 256 + hi)
            mms([(pv, A("BM"), sub(LV, lo, hi))])
            tt(A("h2", lo, hi), pv, A("Bz", lo, hi), O.add)
            ts(A("h2", lo, hi), A("h2", lo, hi), 255, O.bitwise_and)
            ts(A("HH", lo, hi), A("h2", lo, hi), A("cls", t, t + 1), O.add)
            for m in range(3):
                s = (t + 1 + m) & 3
                J = A(("P2", "P3", "P7")[m], lo, hi)
                tag[0] = "look%d%d" % (m, h)
                mms([(J, A("SEL", 128 * m, 128 * m + 128), A("HH", lo, hi))])
                tag[0] = "list"
                lin(A("HB", 256 * m + lo, 256 * m + hi), J, 0.25, -0.25 * (s + 1))
                tag[0] = "look%d%d" % (m, h)
                look(A("OFF", 256 * m + lo, 256 * m + hi), A("DS", lo, hi), sub(S, lo, hi), J)
        tag[0] = "list"
        mms([(A("P6", 0, 48), W(y), A("HB", y, 768, 16)) for y in range(16)])
        ts(A("Lf"), A("P6", 0, 48), 0.0625, O.mult)
        cp(A("LV"), A("Lf"))
        tt(A("PAY"), A("Lf"), A("PAYc"), O.add)
        if t == 0:
            first_worth(1)
            first_worth(3)
            tag[0] = "rb"
            send(back(1), far[0], A("C3"), "rb0")
            send(back(1), far[1], A("V3"), "rv0")
            first_worth(2)
        tag[0] = "vj2"
        recv(A("TB%d" % (t + 1)), "rt%d" % t, helper(ahead(t + 1)) if t else ahead(1), CP["tab"] * (t + 1))
        recv(far[0], "rb%d" % t, ahead(t + 1))
        recv(far[1], "rv%d" % t, ahead(t + 1))
        if t > 0:
            recv(sub(home[t - 1][0], 0, 256), "bb%d" % (t - 1), back(t))
            recv(sub(home[t - 1][1], 0, 256), "bv%d" % (t - 1), back(t))
        def eb(m, k):
            return 6144 * (k >> 3) + 256 * (8 * m + (k & 7))

        for m in range(3):
            tag[0] = "dd%d" % m
            for k in range(16):
                ts(A("EB", eb(m, k), eb(m, k) + 256 - 16 * k), A("HB", 256 * m + 16 * k, 256 * m + 256), A("Lf", 16 * m + k, 16 * m + k + 1), O.is_equal)
            for h in range(2):
                l = []
                for k in range(8 * h + 7):
                    a = max(128 * h, 16 * k + 16)
                    l.append((A("P%d" % h, 128 * (m - h) + a, 128 * m + 128), A("BM8"), A("EB", eb(m, k) + a - 16 * k, eb(m, k) + 128 * h + 128 - 16 * k)))
                if h == 0:
                    l.insert(0, (A("P0", 128 * m, 128 * m + 16), A("BM8"), A("ZR")))
                for k in range(0, len(l), 4):
                    mms(l[k:k + 4], ("P", t, h), False)
                    if k == 0:
                        ops[-1]["use"].append((A("P%d" % h, 128 * m, 128 * m + 128), 1))
            tag[0] = "vj%d" % m
            move(A("VJ", 256 * m, 256 * m + 256), IND(A("VM", wa + slot[m], wa + slot[m] + 256), A("LV", 16 * m, 16 * m + 16)))
            for h in range(2):
                mms([(A("P%d" % h, 128 * m, 128 * m + 128), A("BMn"), A("VJ", 256 * m + 128 * h, 256 * m + 128 * h + 128))], ("P", t, h), False)
        tag[0] = "dd2"
        for h in range(2):
            for x in range(1, 16, 5):
                mms([(A("P%d" % h, j, 369 + j, 16), A("TRI", 128 * j, 128 * j + 128), A("EB", 6144 * h + j, 6144 * h + j + 23 * 256 + 1, 256))
                     for j in range(x, x + 5)], ("P", t, h), False)
        win, vwin = A("BW", wa, wa + 1024), A("VM", wa, wa + 1024)
        for h in range(2):
            lo, hi, SM, P = 128 * h, 128 * h + 128, "SM%d" % h, "P%d" % h
            for m in range(3):
                tag[0] = "j%d%d" % (m, h)
                for a in range(0, 128, CH):
                    b = 2048 * (2 - m) + 16 * a
                    sights("TB%d" % (t + 1 if m == 2 else 0), "OFF", 256 * m + lo + a, SM, b, 1)
                    mms([(A(P, 128 * m + a, 128 * m + a + CH), W(d), A(SM, b + d, b + 16 * CH, 16)) for d in range(16)], ("P", t, h), False)
                    ops[-1]["tag"] += "s"
            tag[0] = "dec%d" % h
            C = [A("CM", 256 * m + lo, 256 * m + hi) for m in range(3)]
            for m in range(3):
                ts(C[m], A(P, 128 * m, 128 * m + 128), 0.0, O.is_gt, 8192.0, O.mult)
                ops[-1]["use"].append((A(P, 0, 384), 0))
            E = A("P6", 64 + 64 * h, 112 + 64 * h)
            mms([(E, W(y), A("CM", y, 768, 16)) for y in range(16)])
            Q, Rr = A("P5", 0, 128), A("P5", 128, 256)
            mms([(Rr, A("BID"), C[m]) for m in range(3)])
            mms([(Q, A("NSH"), C[m]) for m in range(3)])
            tt(A("KS", 0, 48), E, A("PAY"), O.add)
            tt(A("K1"), A("KS", 0, 32), A("KS", 32, 64), O.max)
            kb = A("KB", 32, 40)
            tt(kb, A("K1", 8 * h, 8 * h + 8), A("K1", 16 + 8 * h, 24 + 8 * h), O.max)
            ts(A("KB", 16 * h, 16 * h + 8), kb, 1023, O.bitwise_and)
            cp(A("IDX", 16 * h, 16 * h + 8), A("KB", 16 * h, 16 * h + 8))
            ts(A("KB", 16 * h + 8, 16 * h + 16), kb, 13, O.arith_shift_right)
            ts(A("KB", 40, 48), kb, 6144, O.bitwise_and)
            tt(A("KB", 40, 48), A("KB", 40, 48), A("KB", 16 * h + 8, 16 * h + 16), O.add)
            cp(A("IDX", 16 * h + 8, 16 * h + 16), A("KB", 40, 48))
            iu, iv = A("IDX", 16 * h, 16 * h + 8), A("IDX", 16 * h + 8, 16 * h + 16)
            U = A("UB%d" % t, lo, hi)
            tag[0] = "ys%d" % h
            lin(A("Ys", lo, hi), sub(LB, lo, hi), 1.0, -2344.0)
            ts(Rr, Rr, A("col", 6, 7), O.is_gt)
            tt(A("PS%d" % t, lo, hi), Rr, A("Ys", lo, hi), O.mult)
            tag[0] = "sc%d" % h
            tt(A("XS", lo, hi), Q, sub(S, lo, hi), O.add)
            move(U, IND(win, iu))
            move(A("SMg", lo, hi), IND(A(SM), iv))
            cp(IND(win, iu), A("XS", lo, hi))
            cp(IND(vwin, iu), A("SMg", lo, hi))
            tag[0] = "rp"
            send(ahead(1), A("PL%d" % t, lo, hi), A("PS%d" % t, lo, hi), "r%s%d" % ("pq"[h], t))
            if h == 1:
                tag[0] = "bb"
                send(ahead(t + 1), sub(home[t][1], 0, 256), far[1], "bv%d" % t)
                send(ahead(t + 1), sub(home[t][0], 0, 256), far[0], "bb%d" % t, [sent["bv%d" % t]] if t + 1 < RO else [])
            tag[0] = "own%d" % h
            mine(U, t, lo, 128, A("P%d" % (5 + h), 256, 384), "OFFO", lo, A("VU%d" % t, lo, hi), 16 * lo)
        if t + 1 < RO:
            tag[0] = "rb"
            a = wa + 768 + slot[2]
            send(back(t + 2), A("BW", a, a + 256), A("UB%d" % t), "rb%d" % (t + 1), [sent["bb%d" % t]])
            send(back(t + 2), A("VM", a, a + 256), A("VU%d" % t), "rv%d" % (t + 1))

    tag[0] = "out"
    last = RO - 1
    recv(A("PL%d" % last, 0, 128), "rp%d" % last, back(1))
    recv(A("PL%d" % last, 128, 256), "rq%d" % last, back(1))
    recv(A("C1b"), "bb%d" % last, back(RO))
    recv(A("V1b"), "bv%d" % last, back(RO))
    fin = [home[1], home[2], (("UB2", 0), ("VU2", 0)), home[0]]
    g8 = slice(0, 8)
    mms([(A("P3", 0, 256, 1, g8), A("G8f"), A("PL%d" % last))])
    ts(A("PO", 0, 256, 1, g8), A("P3", 0, 256, 1, g8), 2344.0 - 296.0, O.add, -1.0, O.max)
    dma("S", hbm(T.yp[:]), A("PO", 0, 256, 1, g8))
    for s in range(4):
        ts(A("OUT", s, 1021 + s, 4), sub(fin[s][0], 0, 256), -296.0, O.add, -1.0, O.max)
        pv = A("P%d" % (s & 1), 256 * (s >> 1), 256 * (s >> 1) + 256, 1, g8)
        mms([(pv, A("G8"), sub(fin[s][1], 0, 256))])
        move(A("OUTV", s, 1021 + s, 4, g8), pv)
    dma("Y", hbm(T.yb[:]), A("OUT"))
    dma("Y", hbm(T.yv[:]), A("OUTV", 0, 1024, 1, g8))

    if not _order:
        _order["o"] = arrange(ops, needs(ops))
    for i, q in _order["o"]:
        issue(ops[i], q)
    for s in sorted(cnt):
        if cnt[s]:
            g.wait_ge(T.sem[s], cnt[s])
